import numpy as np
import ml_dtypes


def mxq(x, axis, fmt="e4m3"):
    dtype, down = {"e4m3": (ml_dtypes.float8_e4m3fn, 7), "e5m2": (ml_dtypes.float8_e5m2, 14)}[fmt]
    v = np.moveaxis(np.asarray(x, np.float32).astype(ml_dtypes.bfloat16).astype(np.float64), axis, -1)
    blocks = v.reshape(v.shape[:-1] + (-1, 32))
    amax = np.abs(blocks).max(-1, keepdims=True)
    byte = np.maximum(np.where(amax > 0, np.frexp(amax)[1] - 1 + 127, 0) - down, 1)
    scale = np.exp2(byte - 127.0)
    codes = (blocks / scale).astype(np.float32).astype(dtype).astype(np.float64)
    return np.moveaxis((codes * scale).reshape(v.shape), -1, axis)


WIDE = False


def mx_kscale(k):
    if not WIDE:
        return np.ones(k)
    levels = np.array([10, -10, 5, -5, 0])
    if k % 512:
        return np.exp2(np.random.permutation(np.resize(levels, k // 32))).repeat(32)
    a = np.empty((k // 512, 16))
    for p in range(k // 512):
        a[p, :8] = np.random.permutation(np.resize(levels, 8))
        for g in range(8):
            far = levels[np.abs(levels - a[p, g]) >= 10]
            a[p, g + 8] = far[np.random.randint(len(far))]
    return np.exp2(a.ravel()).repeat(32)


def f64(x):
    return np.asarray(x).astype(np.float64)


def striped(idx):
    return np.tile(idx.reshape(-1, 16).T, (8, 1)).astype(np.uint16)


def unstriped(offs):
    return offs[:16].T.reshape(-1).astype(np.int64)


def striped8(idx):
    return np.concatenate([x.reshape(-1, 16).T for x in idx]).astype(np.uint16)


def runs(offs, k):
    lists = np.stack([offs[16 * r : 16 * r + 16].T.reshape(-1) for r in range(8)]).astype(np.int64)
    return lists[np.arange(k) % 512 // 64]


def pack_weight(w):
    k, n = w.shape
    w = f64(np.asarray(w, np.float32).astype(ml_dtypes.bfloat16)).reshape(k // 32, 32, n)
    amax = np.abs(w).max(1)
    byte = np.clip(np.where(amax > 0, np.frexp(amax)[1] - 1 + 127 - 7, 1), 1, 254)
    scaled = (w * np.exp2(127.0 - byte)[:, None, :]).reshape(k, n).astype(np.float32)
    words = np.ascontiguousarray(scaled.reshape(k // 512, 128, 4, n).transpose(0, 1, 3, 2)).astype(ml_dtypes.float8_e4m3fn).view(np.uint8)
    return words, np.ascontiguousarray(byte.astype(np.uint8).reshape(k // 512, 16, n))


def unpack_weight(words, scales):
    g, p, n, _ = words.shape
    vals = np.ascontiguousarray(words).view(ml_dtypes.float8_e4m3fn).astype(np.float64) * np.repeat(np.exp2(scales.astype(np.float64) - 127.0), 8, axis=1)[..., None]
    return vals.transpose(0, 1, 3, 2).reshape(g * 512, n)


def relu(v):
    return np.maximum(v, 0.0)

def planes(y):
    n, m = y.shape
    v = y.astype(np.float32).astype(ml_dtypes.bfloat16).astype(np.float64).reshape(n // 32, 32, m)
    top = np.abs(v).max(1)
    byte = np.clip(np.where(top > 0, np.frexp(top)[1] - 1 + 127 - 7, 1), 1, 254)
    codes = (v * np.exp2(127.0 - byte)[:, None, :]).reshape(n, m).astype(np.float32).astype(ml_dtypes.float8_e4m3fn).view(np.uint8)
    words = codes.reshape(n // 512, 128, 4, m).transpose(0, 1, 3, 2)
    return np.ascontiguousarray(words), np.ascontiguousarray(byte.astype(np.uint8).reshape(n // 512, 16, m))


K, T, S, V, N, H = 512, 2048, 512, 256, 512, 512


def setup_inputs():
    n = np.random.standard_normal
    s = mx_kscale(K)[:, None]
    u = mx_kscale(S)
    packed_xT = pack_weight(n((K, T)) * s)
    packed_w1 = pack_weight(n((S, N)) / np.sqrt(S) / u[:, None])
    perm = np.stack([np.random.permutation(H) for _ in range(8)])
    return {
        "x_words": packed_xT[0],
        "x_scales": packed_xT[1],
        "wa": (n((K, H)) / np.sqrt(K) / s).astype(np.float32),
        "gt": (np.random.uniform(0.5, 1.5, (S, 1)) * u[:, None]).astype(np.float32),
        "w1_words": packed_w1[0],
        "w1_scales": packed_w1[1],
        "offs": striped(np.random.permutation(T)[:S]),
        "la": striped8(perm[:, :V]),
        "lb": striped8(perm[:, V:]),
    }


def reference(x_words, x_scales, wa, gt, w1_words, w1_scales, offs, la, lb):
    xq = unpack_weight(x_words, x_scales)[:, unstriped(offs)]
    y = xq.T @ mxq(f64(wa), 0, "e4m3")
    a = y[np.arange(S)[:, None], runs(la, S)]
    b = y[np.arange(S)[:, None], runs(lb, S)]
    mx = np.maximum(a, b)
    mn = np.minimum(a, b)
    p = np.zeros((S, H))
    p[np.arange(S)[:, None], runs(la, S)] = mn
    zs = p.copy()
    zs[np.arange(S)[:, None], runs(lb, S)] = mx
    z = f64(gt) * relu(zs)
    out_0 = unpack_weight(w1_words, w1_scales).T @ mxq(z, 0, "e4m3")
    return (out_0,) + planes(out_0)

@@ -1,0 +1,207 @@
+from contextlib import ExitStack
+
+import concourse.mybir as mybir
+
+K, T, S, V, N, H = 512, 2048, 512, 256, 512, 512
+FLOPS = 2 * K * S * H + 2 * S * N * H
+
+F32 = mybir.dt.float32
+BF16 = mybir.dt.bfloat16
+I32 = mybir.dt.int32
+U32 = mybir.dt.uint32
+U16 = mybir.dt.uint16
+U8 = mybir.dt.uint8
+FP8X4 = mybir.dt.float8_e4m3fn_x4
+ALU = mybir.AluOpType
+ACT = mybir.ActivationFunctionType
+
+P = 128
+PACK = 4
+QUADS = 4
+CW = 128
+WA_FIRST = 384
+SLOT_ORDER = (2, 0, 1, 3)
+
+
+def load_scale_rows(queue, plane, rows):
+    for quad in range(QUADS):
+        queue.dma_start(out=plane[32 * quad : 32 * quad + 4, :].bitcast(I32), in_=rows[4 * quad : 4 * quad + 4, :].bitcast(I32))
+
+
+def interleave_views(grouped, planes):
+    return (
+        grouped.rearrange("p (c i) t -> p c t i", i=4),
+        planes.rearrange("p t (c i) -> p c t i", i=4),
+    )
+
+
+def tile_picked_mixscat_relu_po_kernel(
+    tc, x_words, x_scales, wa, gt, w1_words, w1_scales, offs, la, lb, out_0, out_1, out_2
+):
+    nc = tc.nc
+    with ExitStack() as ctx:
+        keep = ctx.enter_context(tc.tile_pool(name="keep", bufs=1))
+        ring = ctx.enter_context(tc.tile_pool(name="ring", bufs=3))
+        psum = ctx.enter_context(tc.psum_pool(name="psum", bufs=8))
+
+        offs_sb = keep.tile([P, S // 16], U16, name="offs_sb")
+        la_sb = keep.tile([P, V // 16], U16, name="la_sb")
+        lb_sb = keep.tile([P, V // 16], U16, name="lb_sb")
+        xw = keep.tile([P, T], I32, name="xw", align_bytes=64)
+        xs = keep.tile([P, T], U8, name="xs", align_bytes=64)
+        wa_first = keep.tile([P, PACK, WA_FIRST], F32, name="wa_first", align_bytes=64)
+        wa_last = keep.tile([P, PACK, H - WA_FIRST], F32, name="wa_last", align_bytes=64)
+        gt_sb = keep.tile([P, PACK], F32, name="gt_sb", align_bytes=64)
+        w1w = keep.tile([P, N], I32, name="w1w", align_bytes=64)
+        w1s = keep.tile([P, N], U8, name="w1s", align_bytes=64)
+
+        nc.vector.memset(xs[:].bitcast(I32), 0)
+        nc.vector.memset(w1s[:].bitcast(I32), 0)
+        wa_rows = wa.rearrange("(p t) c -> p t c", t=PACK)
+        nc.sync.dma_start(offs_sb[:], offs)
+        nc.sync.dma_start(out=xw[:], in_=x_words[0].rearrange("p c t -> p (c t)").bitcast(I32))
+        load_scale_rows(nc.sync, xs, x_scales[0])
+        nc.sync.dma_start(out=wa_first[:], in_=wa_rows[:, :, :WA_FIRST])
+        nc.sync.dma_start(out=wa_last[:], in_=wa_rows[:, :, WA_FIRST:])
+        nc.sync.dma_start(la_sb[:], la)
+        nc.sync.dma_start(lb_sb[:], lb)
+        nc.sync.dma_start(out=gt_sb[:], in_=gt.rearrange("(p t) o -> p (t o)", t=PACK))
+        nc.sync.dma_start(out=w1w[:], in_=w1_words[0].rearrange("p c t -> p (c t)").bitcast(I32))
+        load_scale_rows(nc.sync, w1s, w1_scales[0])
+
+        xs_picked = keep.tile([P, S], U8, name="xs_picked", align_bytes=64)
+        xs_dealt = keep.tile([P, S], U8, name="xs_dealt", align_bytes=64)
+        xw_dealt = keep.tile([P, S], I32, name="xw_dealt", align_bytes=64)
+        nc.vector.tensor_copy(xs_picked[:], xs[:].indirect(offs_sb[:]))
+        nc.vector.tensor_copy(
+            xs_dealt[:].rearrange("p (t m) -> p m t", t=PACK), xs_picked[:].rearrange("p (m t) -> p m t", t=PACK)
+        )
+        nc.vector.tensor_copy(
+            xw_dealt[:].bitcast(U32).rearrange("p (t m) -> p m t", t=PACK), xw[:].bitcast(U32).indirect(offs_sb[:])
+        )
+
+        wa_codes = keep.tile([P, H], I32, name="wa_codes", align_bytes=64)
+        wa_scales = keep.tile([P, H], U8, name="wa_scales", align_bytes=64)
+        pieces = (
+            (nc.scalar.copy, wa_first[:, :, :CW], slice(0, CW)),
+            (nc.scalar.copy, wa_first[:, :, CW : 2 * CW], slice(CW, 2 * CW)),
+            (nc.vector.tensor_copy, wa_first[:, :, 2 * CW :], slice(2 * CW, WA_FIRST)),
+            (nc.vector.tensor_copy, wa_last[:], slice(WA_FIRST, H)),
+        )
+        groups = []
+        for index, (cast, planes, cols) in enumerate(pieces):
+            grouped = keep.tile([P, cols.stop - cols.start, PACK], BF16, name="wa_grouped%d" % index, align_bytes=64)
+            cast(*interleave_views(grouped[:], planes))
+            groups.append(grouped)
+        for grouped, (cast, planes, cols) in zip(groups, pieces):
+            nc.vector.quantize_mx(
+                out=wa_codes[:, cols].bitcast(FP8X4), scales=wa_scales[:, cols], in_=grouped[:].rearrange("p c t -> p (c t)")
+            )
+
+        def project(slot, y_sb, col_groups):
+            rows = slice(slot * P, (slot + 1) * P)
+            for col_list in col_groups:
+                first, last = col_list[0].start, col_list[-1].stop
+                bank = psum.tile([P, last - first], F32, name="bank", tag="bank")
+                for cols in col_list:
+                    nc.tensor.matmul_mx(
+                        out=bank[:, cols.start - first : cols.stop - first],
+                        lhsT=xw_dealt[:, rows].bitcast(FP8X4),
+                        lhsT_scale=xs_dealt[:, rows],
+                        rhs=wa_codes[:, cols].bitcast(FP8X4),
+                        rhs_scale=wa_scales[:, cols],
+                        start=True,
+                        stop=True,
+                    )
+                nc.scalar.activation(y_sb[:, first:last], bank[:], ACT.Relu)
+
+        piece_cols = [cols for cast, planes, cols in pieces]
+        y_tiles = {}
+        for step, slot in enumerate(SLOT_ORDER):
+            y_tiles[slot] = keep.tile([P, H], F32, name="y%d" % slot)
+            project(slot, y_tiles[slot], [piece_cols[:3], piece_cols[3:]] if step == 0 else [[slice(0, H)]])
+
+        w1w_dealt = keep.tile([P, N], I32, name="w1w_dealt", align_bytes=64)
+        w1s_dealt = keep.tile([P, N], U8, name="w1s_dealt", align_bytes=64)
+
+        chunks = H // CW
+        z_grouped = [keep.tile([P, CW, PACK], BF16, name="z_grouped%d" % q, align_bytes=64) for q in range(chunks)]
+
+        def fetch(slot):
+            a = keep.tile([P, V], F32, name="a%d" % slot)
+            d = keep.tile([P, V], F32, name="d%d" % slot)
+            up = keep.tile([P, V], F32, name="up%d" % slot)
+            drop = keep.tile([P, V], F32, name="drop%d" % slot)
+            down = keep.tile([P, V], F32, name="down%d" % slot)
+            nc.vector.tensor_copy(a[:], y_tiles[slot][:].indirect(la_sb[:]))
+            nc.vector.tensor_tensor(d[:], y_tiles[slot][:].indirect(lb_sb[:]), a[:], ALU.subtract)
+            nc.scalar.activation(up[:], d[:], ACT.Relu)
+            nc.scalar.activation(drop[:], d[:], ACT.Relu, scale=-1.0)
+            nc.scalar.activation(down[:], drop[:], ACT.Copy, scale=-1.0)
+            return a, up, down
+
+        def put(slot, a, up, down):
+            zs = ring.tile([P, H], F32, name="zs")
+            nc.vector.tensor_tensor(zs[:].indirect(lb_sb[:]), a[:], up[:], ALU.add)
+            nc.vector.tensor_tensor(zs[:].indirect(la_sb[:]), a[:], down[:], ALU.add)
+            for q in range(chunks):
+                cols = slice(q * CW, (q + 1) * CW)
+                if slot == SLOT_ORDER[-1] and q < chunks // 2:
+                    nc.vector.tensor_scalar(z_grouped[q][:, :, slot], zs[:, cols], gt_sb[:, slot : slot + 1], None, ALU.mult)
+                else:
+                    nc.scalar.activation(z_grouped[q][:, :, slot], zs[:, cols], ACT.Copy, scale=gt_sb[:, slot : slot + 1])
+
+        fetched = fetch(SLOT_ORDER[0])
+        for step, slot in enumerate(SLOT_ORDER):
+            ahead = fetch(SLOT_ORDER[step + 1]) if step + 1 < PACK else None
+            if step == 0:
+                nc.vector.tensor_copy(
+                    w1w_dealt[:].rearrange("p (t m) -> p m t", t=PACK), w1w[:].rearrange("p (m t) -> p m t", t=PACK)
+                )
+                nc.vector.tensor_copy(
+                    w1s_dealt[:].rearrange("p (t m) -> p m t", t=PACK), w1s[:].rearrange("p (m t) -> p m t", t=PACK)
+                )
+            put(slot, *fetched)
+            fetched = ahead
+
+        z_codes = keep.tile([P, H], I32, name="z_codes", align_bytes=64)
+        z_scales = keep.tile([P, H], U8, name="z_scales", align_bytes=64)
+        o_codes = keep.tile([P, H], I32, name="o_codes", align_bytes=64)
+        o_scales = keep.tile([P, H], U8, name="o_scales", align_bytes=64)
+        out_rows = out_0.rearrange("(p t) c -> p t c", t=PACK)
+        out_words = out_1[0].rearrange("p c t -> p (c t)").bitcast(I32)
+        for q in range(chunks):
+            cols = slice(q * CW, (q + 1) * CW)
+            nc.vector.quantize_mx(
+                out=z_codes[:, cols].bitcast(FP8X4), scales=z_scales[:, cols], in_=z_grouped[q][:].rearrange("p c t -> p (c t)")
+            )
+        for q in range(chunks):
+            cols = slice(q * CW, (q + 1) * CW)
+            bank = psum.tile([P, PACK, CW], F32, name="bank", tag="bank")
+            for slot in range(PACK):
+                rows = slice(slot * P, (slot + 1) * P)
+                nc.tensor.matmul_mx(
+                    out=bank[:, slot, :],
+                    lhsT=w1w_dealt[:, rows].bitcast(FP8X4),
+                    lhsT_scale=w1s_dealt[:, rows],
+                    rhs=z_codes[:, cols].bitcast(FP8X4),
+                    rhs_scale=z_scales[:, cols],
+                    start=True,
+                    stop=True,
+                )
+            o_sb = keep.tile([P, PACK, CW], F32, name="o_sb%d" % q, align_bytes=64)
+            o_grouped = keep.tile([P, CW, PACK], BF16, name="o_grouped%d" % q, align_bytes=64)
+            nc.scalar.copy(o_sb[:], bank[:])
+            nc.sync.dma_start(out=out_rows[:, :, cols], in_=o_sb[:])
+            nc.vector.tensor_copy(*interleave_views(o_grouped[:], o_sb[:]))
+            nc.vector.quantize_mx(
+                out=o_codes[:, cols].bitcast(FP8X4), scales=o_scales[:, cols], in_=o_grouped[:].rearrange("p c t -> p (c t)")
+            )
+            if q % 2 == 1:
+                half = slice((q - 1) * CW, (q + 1) * CW)
+                nc.sync.dma_start(out=out_words[:, half], in_=o_codes[:, half])
+        for quad in range(QUADS):
+            queue = nc.scalar if quad % 2 == 0 else nc.sync
+            queue.dma_start(
+                out=out_2[0, 4 * quad : 4 * quad + 4, :].bitcast(I32), in_=o_scales[32 * quad : 32 * quad + 4, :].bitcast(I32)
+            )

@@ -19,7 +19,7 @@ P = 128
 PACK = 4
 QUADS = 4
 CW = 128
-WA_FIRST = 384
+WA_FIRST = 256
 SLOT_ORDER = (2, 0, 1, 3)
 
 
@@ -50,7 +50,8 @@ def tile_picked_mixscat_relu_po_kernel(
         xw = keep.tile([P, T], I32, name="xw", align_bytes=64)
         xs = keep.tile([P, T], U8, name="xs", align_bytes=64)
         wa_first = keep.tile([P, PACK, WA_FIRST], F32, name="wa_first", align_bytes=64)
-        wa_last = keep.tile([P, PACK, H - WA_FIRST], F32, name="wa_last", align_bytes=64)
+        wa_mid = keep.tile([P, PACK, CW], F32, name="wa_mid", align_bytes=64)
+        wa_last = keep.tile([P, PACK, CW], F32, name="wa_last", align_bytes=64)
         gt_sb = keep.tile([P, PACK], F32, name="gt_sb", align_bytes=64)
         w1w = keep.tile([P, N], I32, name="w1w", align_bytes=64)
         w1s = keep.tile([P, N], U8, name="w1s", align_bytes=64)
@@ -59,15 +60,16 @@ def tile_picked_mixscat_relu_po_kernel(
         nc.vector.memset(w1s[:].bitcast(I32), 0)
         wa_rows = wa.rearrange("(p t) c -> p t c", t=PACK)
         nc.sync.dma_start(offs_sb[:], offs)
-        nc.sync.dma_start(out=xw[:], in_=x_words[0].rearrange("p c t -> p (c t)").bitcast(I32))
-        load_scale_rows(nc.sync, xs, x_scales[0])
         nc.sync.dma_start(out=wa_first[:], in_=wa_rows[:, :, :WA_FIRST])
-        nc.sync.dma_start(out=wa_last[:], in_=wa_rows[:, :, WA_FIRST:])
+        load_scale_rows(nc.sync, xs, x_scales[0])
+        nc.sync.dma_start(out=xw[:], in_=x_words[0].rearrange("p c t -> p (c t)").bitcast(I32))
+        nc.sync.dma_start(out=wa_mid[:], in_=wa_rows[:, :, WA_FIRST : WA_FIRST + CW])
+        nc.sync.dma_start(out=wa_last[:], in_=wa_rows[:, :, WA_FIRST + CW :])
+        nc.sync.dma_start(out=w1w[:], in_=w1_words[0].rearrange("p c t -> p (c t)").bitcast(I32))
         nc.sync.dma_start(la_sb[:], la)
         nc.sync.dma_start(lb_sb[:], lb)
-        nc.sync.dma_start(out=gt_sb[:], in_=gt.rearrange("(p t) o -> p (t o)", t=PACK))
-        nc.sync.dma_start(out=w1w[:], in_=w1_words[0].rearrange("p c t -> p (c t)").bitcast(I32))
         load_scale_rows(nc.sync, w1s, w1_scales[0])
+        nc.sync.dma_start(out=gt_sb[:], in_=gt.rearrange("(p t) o -> p (t o)", t=PACK))
 
         xs_picked = keep.tile([P, S], U8, name="xs_picked", align_bytes=64)
         xs_dealt = keep.tile([P, S], U8, name="xs_dealt", align_bytes=64)
@@ -85,8 +87,8 @@ def tile_picked_mixscat_relu_po_kernel(
         pieces = (
             (nc.scalar.copy, wa_first[:, :, :CW], slice(0, CW)),
             (nc.scalar.copy, wa_first[:, :, CW : 2 * CW], slice(CW, 2 * CW)),
-            (nc.vector.tensor_copy, wa_first[:, :, 2 * CW :], slice(2 * CW, WA_FIRST)),
-            (nc.vector.tensor_copy, wa_last[:], slice(WA_FIRST, H)),
+            (nc.scalar.copy, wa_mid[:], slice(2 * CW, 3 * CW)),
+            (nc.scalar.copy, wa_last[:], slice(3 * CW, H)),
         )
         groups = []
         for index, (cast, planes, cols) in enumerate(pieces):
@@ -127,23 +129,38 @@ def tile_picked_mixscat_relu_po_kernel(
         chunks = H // CW
         z_grouped = [keep.tile([P, CW, PACK], BF16, name="z_grouped%d" % q, align_bytes=64) for q in range(chunks)]
 
-        def fetch(slot):
-            a = keep.tile([P, V], F32, name="a%d" % slot)
-            d = keep.tile([P, V], F32, name="d%d" % slot)
-            up = keep.tile([P, V], F32, name="up%d" % slot)
-            drop = keep.tile([P, V], F32, name="drop%d" % slot)
-            down = keep.tile([P, V], F32, name="down%d" % slot)
-            nc.vector.tensor_copy(a[:], y_tiles[slot][:].indirect(la_sb[:]))
-            nc.vector.tensor_tensor(d[:], y_tiles[slot][:].indirect(lb_sb[:]), a[:], ALU.subtract)
-            nc.scalar.activation(up[:], d[:], ACT.Relu)
-            nc.scalar.activation(drop[:], d[:], ACT.Relu, scale=-1.0)
-            nc.scalar.activation(down[:], drop[:], ACT.Copy, scale=-1.0)
-            return a, up, down
+        a_tiles, d_tiles, up_tiles, down_tiles, zs_tiles = {}, {}, {}, {}, {}
+        halves = [(slice(h * V // 2, (h + 1) * V // 2), slice(h * V // 32, (h + 1) * V // 32)) for h in range(2)]
 
-        def put(slot, a, up, down):
-            zs = ring.tile([P, H], F32, name="zs")
-            nc.vector.tensor_tensor(zs[:].indirect(lb_sb[:]), a[:], up[:], ALU.add)
-            nc.vector.tensor_tensor(zs[:].indirect(la_sb[:]), a[:], down[:], ALU.add)
+        def fetch(slot):
+            a_tiles[slot] = keep.tile([P, V], F32, name="a%d" % slot)
+            d_tiles[slot] = keep.tile([P, V], F32, name="d%d" % slot)
+            for entries, offsets in halves:
+                nc.vector.tensor_copy(a_tiles[slot][:, entries], y_tiles[slot][:].indirect(la_sb[:, offsets]))
+            for entries, offsets in halves:
+                nc.vector.tensor_tensor(
+                    d_tiles[slot][:, entries], y_tiles[slot][:].indirect(lb_sb[:, offsets]), a_tiles[slot][:, entries], ALU.subtract
+                )
+
+        def rise(slot):
+            up_tiles[slot] = keep.tile([P, V], F32, name="up%d" % slot)
+            nc.scalar.activation(up_tiles[slot][:], d_tiles[slot][:], ACT.Relu)
+
+        def fall(slot):
+            drop = keep.tile([P, V], F32, name="drop%d" % slot)
+            down_tiles[slot] = keep.tile([P, V], F32, name="down%d" % slot)
+            nc.scalar.activation(drop[:], d_tiles[slot][:], ACT.Relu, scale=-1.0)
+            nc.scalar.activation(down_tiles[slot][:], drop[:], ACT.Copy, scale=-1.0)
+
+        def put_larger(slot):
+            zs_tiles[slot] = ring.tile([P, H], F32, name="zs")
+            nc.vector.tensor_tensor(zs_tiles[slot][:].indirect(lb_sb[:]), a_tiles[slot][:], up_tiles[slot][:], ALU.add)
+
+        def put_smaller(slot):
+            nc.vector.tensor_tensor(zs_tiles[slot][:].indirect(la_sb[:]), a_tiles[slot][:], down_tiles[slot][:], ALU.add)
+
+        def weigh(slot):
+            zs = zs_tiles[slot]
             for q in range(chunks):
                 cols = slice(q * CW, (q + 1) * CW)
                 if slot == SLOT_ORDER[-1] and q < chunks // 2:
@@ -151,18 +168,35 @@ def tile_picked_mixscat_relu_po_kernel(
                 else:
                     nc.scalar.activation(z_grouped[q][:, :, slot], zs[:, cols], ACT.Copy, scale=gt_sb[:, slot : slot + 1])
 
-        fetched = fetch(SLOT_ORDER[0])
-        for step, slot in enumerate(SLOT_ORDER):
-            ahead = fetch(SLOT_ORDER[step + 1]) if step + 1 < PACK else None
-            if step == 0:
-                nc.vector.tensor_copy(
-                    w1w_dealt[:].rearrange("p (t m) -> p m t", t=PACK), w1w[:].rearrange("p (m t) -> p m t", t=PACK)
-                )
-                nc.vector.tensor_copy(
-                    w1s_dealt[:].rearrange("p (t m) -> p m t", t=PACK), w1s[:].rearrange("p (m t) -> p m t", t=PACK)
-                )
-            put(slot, *fetched)
-            fetched = ahead
+        for slot in SLOT_ORDER:
+            fetch(slot)
+        nc.vector.tensor_copy(
+            w1w_dealt[:].rearrange("p (t m) -> p m t", t=PACK), w1w[:].rearrange("p (m t) -> p m t", t=PACK)
+        )
+        nc.vector.tensor_copy(
+            w1s_dealt[:].rearrange("p (t m) -> p m t", t=PACK), w1s[:].rearrange("p (m t) -> p m t", t=PACK)
+        )
+        first, second, third, last = SLOT_ORDER
+        rise(first)
+        rise(second)
+        fall(first)
+        rise(third)
+        fall(second)
+        rise(last)
+        put_larger(first)
+        put_larger(second)
+        put_smaller(first)
+        put_larger(third)
+        put_smaller(second)
+        weigh(first)
+        fall(third)
+        fall(last)
+        put_larger(last)
+        put_smaller(third)
+        put_smaller(last)
+        weigh(second)
+        weigh(third)
+        weigh(last)
 
         z_codes = keep.tile([P, H], I32, name="z_codes", align_bytes=64)
         z_scales = keep.tile([P, H], U8, name="z_scales", align_bytes=64)
@@ -191,9 +225,12 @@ def tile_picked_mixscat_relu_po_kernel(
                 )
             o_sb = keep.tile([P, PACK, CW], F32, name="o_sb%d" % q, align_bytes=64)
             o_grouped = keep.tile([P, CW, PACK], BF16, name="o_grouped%d" % q, align_bytes=64)
+            if q == chunks - 1:
+                nc.vector.tensor_copy(*interleave_views(o_grouped[:], bank[:]))
             nc.scalar.copy(o_sb[:], bank[:])
             nc.sync.dma_start(out=out_rows[:, :, cols], in_=o_sb[:])
-            nc.vector.tensor_copy(*interleave_views(o_grouped[:], o_sb[:]))
+            if q < chunks - 1:
+                nc.vector.tensor_copy(*interleave_views(o_grouped[:], o_sb[:]))
             nc.vector.quantize_mx(
                 out=o_codes[:, cols].bitcast(FP8X4), scales=o_scales[:, cols], in_=o_grouped[:].rearrange("p c t -> p (c t)")
             )

@@ -19,7 +19,7 @@ P = 128
 PACK = 4
 QUADS = 4
 CW = 128
-WA_FIRST = 256
+X_FIRST = 512
 SLOT_ORDER = (2, 0, 1, 3)
 
 
@@ -49,9 +49,9 @@ def tile_picked_mixscat_relu_po_kernel(
         lb_sb = keep.tile([P, V // 16], U16, name="lb_sb")
         xw = keep.tile([P, T], I32, name="xw", align_bytes=64)
         xs = keep.tile([P, T], U8, name="xs", align_bytes=64)
-        wa_first = keep.tile([P, PACK, WA_FIRST], F32, name="wa_first", align_bytes=64)
-        wa_mid = keep.tile([P, PACK, CW], F32, name="wa_mid", align_bytes=64)
-        wa_last = keep.tile([P, PACK, CW], F32, name="wa_last", align_bytes=64)
+        chunks = H // CW
+        chunk_cols = [slice(q * CW, (q + 1) * CW) for q in range(chunks)]
+        wa_raw = [keep.tile([P, PACK, CW], F32, name="wa_raw%d" % q, align_bytes=64) for q in range(chunks)]
         gt_sb = keep.tile([P, PACK], F32, name="gt_sb", align_bytes=64)
         w1w = keep.tile([P, N], I32, name="w1w", align_bytes=64)
         w1s = keep.tile([P, N], U8, name="w1s", align_bytes=64)
@@ -60,11 +60,13 @@ def tile_picked_mixscat_relu_po_kernel(
         nc.vector.memset(w1s[:].bitcast(I32), 0)
         wa_rows = wa.rearrange("(p t) c -> p t c", t=PACK)
         nc.sync.dma_start(offs_sb[:], offs)
-        nc.sync.dma_start(out=wa_first[:], in_=wa_rows[:, :, :WA_FIRST])
+        nc.sync.dma_start(out=wa_raw[0][:], in_=wa_rows[:, :, chunk_cols[0]])
+        x_rows = x_words[0].rearrange("p c t -> p (c t)").bitcast(I32)
+        nc.sync.dma_start(out=xw[:, :X_FIRST], in_=x_rows[:, :X_FIRST])
         load_scale_rows(nc.sync, xs, x_scales[0])
-        nc.sync.dma_start(out=xw[:], in_=x_words[0].rearrange("p c t -> p (c t)").bitcast(I32))
-        nc.sync.dma_start(out=wa_mid[:], in_=wa_rows[:, :, WA_FIRST : WA_FIRST + CW])
-        nc.sync.dma_start(out=wa_last[:], in_=wa_rows[:, :, WA_FIRST + CW :])
+        nc.sync.dma_start(out=xw[:, X_FIRST:], in_=x_rows[:, X_FIRST:])
+        for q in range(1, chunks):
+            nc.sync.dma_start(out=wa_raw[q][:], in_=wa_rows[:, :, chunk_cols[q]])
         nc.sync.dma_start(out=w1w[:], in_=w1_words[0].rearrange("p c t -> p (c t)").bitcast(I32))
         nc.sync.dma_start(la_sb[:], la)
         nc.sync.dma_start(lb_sb[:], lb)
@@ -72,36 +74,35 @@ def tile_picked_mixscat_relu_po_kernel(
         nc.sync.dma_start(out=gt_sb[:], in_=gt.rearrange("(p t) o -> p (t o)", t=PACK))
 
         xs_picked = keep.tile([P, S], U8, name="xs_picked", align_bytes=64)
-        xs_dealt = keep.tile([P, S], U8, name="xs_dealt", align_bytes=64)
+        xs_first = keep.tile([P, P], U8, name="xs_first", align_bytes=64)
         xw_dealt = keep.tile([P, S], I32, name="xw_dealt", align_bytes=64)
         nc.vector.tensor_copy(xs_picked[:], xs[:].indirect(offs_sb[:]))
-        nc.vector.tensor_copy(
-            xs_dealt[:].rearrange("p (t m) -> p m t", t=PACK), xs_picked[:].rearrange("p (m t) -> p m t", t=PACK)
-        )
+        xs_slots = xs_picked[:].rearrange("p (m t) -> p t m", t=PACK)
+        nc.vector.tensor_copy(xs_first[:], xs_slots[:, SLOT_ORDER[0], :])
         nc.vector.tensor_copy(
             xw_dealt[:].bitcast(U32).rearrange("p (t m) -> p m t", t=PACK), xw[:].bitcast(U32).indirect(offs_sb[:])
         )
 
         wa_codes = keep.tile([P, H], I32, name="wa_codes", align_bytes=64)
         wa_scales = keep.tile([P, H], U8, name="wa_scales", align_bytes=64)
-        pieces = (
-            (nc.scalar.copy, wa_first[:, :, :CW], slice(0, CW)),
-            (nc.scalar.copy, wa_first[:, :, CW : 2 * CW], slice(CW, 2 * CW)),
-            (nc.scalar.copy, wa_mid[:], slice(2 * CW, 3 * CW)),
-            (nc.scalar.copy, wa_last[:], slice(3 * CW, H)),
-        )
         groups = []
-        for index, (cast, planes, cols) in enumerate(pieces):
-            grouped = keep.tile([P, cols.stop - cols.start, PACK], BF16, name="wa_grouped%d" % index, align_bytes=64)
-            cast(*interleave_views(grouped[:], planes))
+        for q in range(chunks):
+            grouped = keep.tile([P, CW, PACK], BF16, name="wa_grouped%d" % q, align_bytes=64)
+            cast = nc.vector.tensor_copy if q == chunks - 1 else nc.scalar.copy
+            cast(*interleave_views(grouped[:], wa_raw[q][:]))
             groups.append(grouped)
-        for grouped, (cast, planes, cols) in zip(groups, pieces):
+        for grouped, cols in zip(groups, chunk_cols):
             nc.vector.quantize_mx(
                 out=wa_codes[:, cols].bitcast(FP8X4), scales=wa_scales[:, cols], in_=grouped[:].rearrange("p c t -> p (c t)")
             )
 
+        xs_dealt = keep.tile([P, S], U8, name="wa_grouped%d" % (chunks - 1), align_bytes=64)
+        nc.vector.tensor_copy(xs_dealt[:, : 2 * P].rearrange("p (t m) -> p m t", t=2), xs_picked[:].rearrange("p (m t) -> p m t", t=PACK)[:, :, 0:2])
+        nc.vector.tensor_copy(xs_dealt[:, 3 * P :], xs_slots[:, 3, :])
+
         def project(slot, y_sb, col_groups):
             rows = slice(slot * P, (slot + 1) * P)
+            row_scales = xs_first[:] if slot == SLOT_ORDER[0] else xs_dealt[:, rows]
             for col_list in col_groups:
                 first, last = col_list[0].start, col_list[-1].stop
                 bank = psum.tile([P, last - first], F32, name="bank", tag="bank")
@@ -109,7 +110,7 @@ def tile_picked_mixscat_relu_po_kernel(
                     nc.tensor.matmul_mx(
                         out=bank[:, cols.start - first : cols.stop - first],
                         lhsT=xw_dealt[:, rows].bitcast(FP8X4),
-                        lhsT_scale=xs_dealt[:, rows],
+                        lhsT_scale=row_scales,
                         rhs=wa_codes[:, cols].bitcast(FP8X4),
                         rhs_scale=wa_scales[:, cols],
                         start=True,
@@ -117,16 +118,18 @@ def tile_picked_mixscat_relu_po_kernel(
                     )
                 nc.scalar.activation(y_sb[:, first:last], bank[:], ACT.Relu)
 
-        piece_cols = [cols for cast, planes, cols in pieces]
         y_tiles = {}
         for step, slot in enumerate(SLOT_ORDER):
-            y_tiles[slot] = keep.tile([P, H], F32, name="y%d" % slot)
-            project(slot, y_tiles[slot], [piece_cols[:3], piece_cols[3:]] if step == 0 else [[slice(0, H)]])
+            if step == 0:
+                y_tiles[slot] = keep.tile([P, H], F32, name="wa_raw%d" % (chunks - 2), align_bytes=64)
+                project(slot, y_tiles[slot], [chunk_cols[:2], chunk_cols[2:3], chunk_cols[3:]])
+            else:
+                y_tiles[slot] = keep.tile([P, H], F32, name="y%d" % slot)
+                project(slot, y_tiles[slot], [[slice(0, H)]])
 
         w1w_dealt = keep.tile([P, N], I32, name="w1w_dealt", align_bytes=64)
         w1s_dealt = keep.tile([P, N], U8, name="w1s_dealt", align_bytes=64)
 
-        chunks = H // CW
         z_grouped = [keep.tile([P, CW, PACK], BF16, name="z_grouped%d" % q, align_bytes=64) for q in range(chunks)]
 
         a_tiles, d_tiles, up_tiles, down_tiles, zs_tiles = {}, {}, {}, {}, {}
@@ -183,20 +186,18 @@ def tile_picked_mixscat_relu_po_kernel(
         rise(third)
         fall(second)
         rise(last)
+        fall(third)
+        fall(last)
         put_larger(first)
         put_larger(second)
         put_smaller(first)
         put_larger(third)
         put_smaller(second)
-        weigh(first)
-        fall(third)
-        fall(last)
         put_larger(last)
         put_smaller(third)
         put_smaller(last)
-        weigh(second)
-        weigh(third)
-        weigh(last)
+        for slot in SLOT_ORDER:
+            weigh(slot)
 
         z_codes = keep.tile([P, H], I32, name="z_codes", align_bytes=64)
         z_scales = keep.tile([P, H], U8, name="z_scales", align_bytes=64)
@@ -211,26 +212,24 @@ def tile_picked_mixscat_relu_po_kernel(
             )
         for q in range(chunks):
             cols = slice(q * CW, (q + 1) * CW)
-            bank = psum.tile([P, PACK, CW], F32, name="bank", tag="bank")
-            for slot in range(PACK):
-                rows = slice(slot * P, (slot + 1) * P)
-                nc.tensor.matmul_mx(
-                    out=bank[:, slot, :],
-                    lhsT=w1w_dealt[:, rows].bitcast(FP8X4),
-                    lhsT_scale=w1s_dealt[:, rows],
-                    rhs=z_codes[:, cols].bitcast(FP8X4),
-                    rhs_scale=z_scales[:, cols],
-                    start=True,
-                    stop=True,
-                )
             o_sb = keep.tile([P, PACK, CW], F32, name="o_sb%d" % q, align_bytes=64)
             o_grouped = keep.tile([P, CW, PACK], BF16, name="o_grouped%d" % q, align_bytes=64)
-            if q == chunks - 1:
-                nc.vector.tensor_copy(*interleave_views(o_grouped[:], bank[:]))
-            nc.scalar.copy(o_sb[:], bank[:])
+            for pair in range(PACK // 2):
+                bank = psum.tile([P, 2, CW], F32, name="bank", tag="bank")
+                for place in range(2):
+                    rows = slice((2 * pair + place) * P, (2 * pair + place + 1) * P)
+                    nc.tensor.matmul_mx(
+                        out=bank[:, place, :],
+                        lhsT=w1w_dealt[:, rows].bitcast(FP8X4),
+                        lhsT_scale=w1s_dealt[:, rows],
+                        rhs=z_codes[:, cols].bitcast(FP8X4),
+                        rhs_scale=z_scales[:, cols],
+                        start=True,
+                        stop=True,
+                    )
+                nc.scalar.copy(o_sb[:, 2 * pair : 2 * pair + 2, :], bank[:])
             nc.sync.dma_start(out=out_rows[:, :, cols], in_=o_sb[:])
-            if q < chunks - 1:
-                nc.vector.tensor_copy(*interleave_views(o_grouped[:], o_sb[:]))
+            nc.vector.tensor_copy(*interleave_views(o_grouped[:], o_sb[:]))
             nc.vector.quantize_mx(
                 out=o_codes[:, cols].bitcast(FP8X4), scales=o_scales[:, cols], in_=o_grouped[:].rearrange("p c t -> p (c t)")
             )

@@ -24,8 +24,8 @@ SLOT_ORDER = (2, 0, 1, 3)
 
 
 def load_scale_rows(queue, plane, rows):
-    for quad in range(QUADS):
-        queue.dma_start(out=plane[32 * quad : 32 * quad + 4, :].bitcast(I32), in_=rows[4 * quad : 4 * quad + 4, :].bitcast(I32))
+    for r in range(PACK):
+        queue.dma_start(out=plane[r:P:32, :].bitcast(I32), in_=rows[r : 4 * QUADS : 4, :].bitcast(I32))
 
 
 def interleave_views(grouped, planes):
@@ -236,8 +236,6 @@ def tile_picked_mixscat_relu_po_kernel(
             if q % 2 == 1:
                 half = slice((q - 1) * CW, (q + 1) * CW)
                 nc.sync.dma_start(out=out_words[:, half], in_=o_codes[:, half])
-        for quad in range(QUADS):
-            queue = nc.scalar if quad % 2 == 0 else nc.sync
-            queue.dma_start(
-                out=out_2[0, 4 * quad : 4 * quad + 4, :].bitcast(I32), in_=o_scales[32 * quad : 32 * quad + 4, :].bitcast(I32)
-            )
+        for r in range(PACK):
+            queue = nc.scalar if r % 2 == 0 else nc.sync
+            queue.dma_start(out=out_2[0, r : 4 * QUADS : 4, :].bitcast(I32), in_=o_scales[r:P:32, :].bitcast(I32))

@@ -41,7 +41,6 @@ def tile_picked_mixscat_relu_po_kernel(
     nc = tc.nc
     with ExitStack() as ctx:
         keep = ctx.enter_context(tc.tile_pool(name="keep", bufs=1))
-        ring = ctx.enter_context(tc.tile_pool(name="ring", bufs=3))
         psum = ctx.enter_context(tc.psum_pool(name="psum", bufs=8))
 
         offs_sb = keep.tile([P, S // 16], U16, name="offs_sb")
@@ -67,18 +66,19 @@ def tile_picked_mixscat_relu_po_kernel(
         nc.sync.dma_start(out=xw[:, X_FIRST:], in_=x_rows[:, X_FIRST:])
         for q in range(1, chunks):
             nc.sync.dma_start(out=wa_raw[q][:], in_=wa_rows[:, :, chunk_cols[q]])
+        load_scale_rows(nc.sync, w1s, w1_scales[0])
         nc.sync.dma_start(out=w1w[:], in_=w1_words[0].rearrange("p c t -> p (c t)").bitcast(I32))
         nc.sync.dma_start(la_sb[:], la)
         nc.sync.dma_start(lb_sb[:], lb)
-        load_scale_rows(nc.sync, w1s, w1_scales[0])
         nc.sync.dma_start(out=gt_sb[:], in_=gt.rearrange("(p t) o -> p (t o)", t=PACK))
 
         xs_picked = keep.tile([P, S], U8, name="xs_picked", align_bytes=64)
-        xs_first = keep.tile([P, P], U8, name="xs_first", align_bytes=64)
+        xs_dealt = keep.tile([P, S], U8, name="xs_dealt", align_bytes=64)
         xw_dealt = keep.tile([P, S], I32, name="xw_dealt", align_bytes=64)
         nc.vector.tensor_copy(xs_picked[:], xs[:].indirect(offs_sb[:]))
-        xs_slots = xs_picked[:].rearrange("p (m t) -> p t m", t=PACK)
-        nc.vector.tensor_copy(xs_first[:], xs_slots[:, SLOT_ORDER[0], :])
+        nc.vector.tensor_copy(
+            xs_dealt[:].rearrange("p (t m) -> p m t", t=PACK), xs_picked[:].rearrange("p (m t) -> p m t", t=PACK)
+        )
         nc.vector.tensor_copy(
             xw_dealt[:].bitcast(U32).rearrange("p (t m) -> p m t", t=PACK), xw[:].bitcast(U32).indirect(offs_sb[:])
         )
@@ -96,13 +96,8 @@ def tile_picked_mixscat_relu_po_kernel(
                 out=wa_codes[:, cols].bitcast(FP8X4), scales=wa_scales[:, cols], in_=grouped[:].rearrange("p c t -> p (c t)")
             )
 
-        xs_dealt = keep.tile([P, S], U8, name="wa_grouped%d" % (chunks - 1), align_bytes=64)
-        nc.vector.tensor_copy(xs_dealt[:, : 2 * P].rearrange("p (t m) -> p m t", t=2), xs_picked[:].rearrange("p (m t) -> p m t", t=PACK)[:, :, 0:2])
-        nc.vector.tensor_copy(xs_dealt[:, 3 * P :], xs_slots[:, 3, :])
-
         def project(slot, y_sb, col_groups):
             rows = slice(slot * P, (slot + 1) * P)
-            row_scales = xs_first[:] if slot == SLOT_ORDER[0] else xs_dealt[:, rows]
             for col_list in col_groups:
                 first, last = col_list[0].start, col_list[-1].stop
                 bank = psum.tile([P, last - first], F32, name="bank", tag="bank")
@@ -110,7 +105,7 @@ def tile_picked_mixscat_relu_po_kernel(
                     nc.tensor.matmul_mx(
                         out=bank[:, cols.start - first : cols.stop - first],
                         lhsT=xw_dealt[:, rows].bitcast(FP8X4),
-                        lhsT_scale=row_scales,
+                        lhsT_scale=xs_dealt[:, rows],
                         rhs=wa_codes[:, cols].bitcast(FP8X4),
                         rhs_scale=wa_scales[:, cols],
                         start=True,
@@ -128,7 +123,7 @@ def tile_picked_mixscat_relu_po_kernel(
                 project(slot, y_tiles[slot], [[slice(0, H)]])
 
         w1w_dealt = keep.tile([P, N], I32, name="w1w_dealt", align_bytes=64)
-        w1s_dealt = keep.tile([P, N], U8, name="w1s_dealt", align_bytes=64)
+        w1s_dealt = keep.tile([P, N], U8, name="wa_grouped%d" % (chunks - 1), align_bytes=64)
 
         z_grouped = [keep.tile([P, CW, PACK], BF16, name="z_grouped%d" % q, align_bytes=64) for q in range(chunks)]
 
@@ -151,12 +146,13 @@ def tile_picked_mixscat_relu_po_kernel(
 
         def fall(slot):
             drop = keep.tile([P, V], F32, name="drop%d" % slot)
-            down_tiles[slot] = keep.tile([P, V], F32, name="down%d" % slot)
+            tag = "zs%d" % SLOT_ORDER[0] if slot == SLOT_ORDER[-1] else "down%d" % slot
+            down_tiles[slot] = keep.tile([P, V], F32, name=tag)
             nc.scalar.activation(drop[:], d_tiles[slot][:], ACT.Relu, scale=-1.0)
             nc.scalar.activation(down_tiles[slot][:], drop[:], ACT.Copy, scale=-1.0)
 
         def put_larger(slot):
-            zs_tiles[slot] = ring.tile([P, H], F32, name="zs")
+            zs_tiles[slot] = keep.tile([P, H], F32, name="zs%d" % slot)
             nc.vector.tensor_tensor(zs_tiles[slot][:].indirect(lb_sb[:]), a_tiles[slot][:], up_tiles[slot][:], ALU.add)
 
         def put_smaller(slot):
@@ -187,7 +183,6 @@ def tile_picked_mixscat_relu_po_kernel(
         fall(second)
         rise(last)
         fall(third)
-        fall(last)
         put_larger(first)
         put_larger(second)
         put_smaller(first)
@@ -195,8 +190,10 @@ def tile_picked_mixscat_relu_po_kernel(
         put_smaller(second)
         put_larger(last)
         put_smaller(third)
+        weigh(first)
+        fall(last)
         put_smaller(last)
-        for slot in SLOT_ORDER:
+        for slot in SLOT_ORDER[1:]:
             weigh(slot)
 
         z_codes = keep.tile([P, H], I32, name="z_codes", align_bytes=64)

@@ -133,9 +133,10 @@ def tile_picked_mixscat_relu_po_kernel(
         def fetch(slot):
             a_tiles[slot] = keep.tile([P, V], F32, name="a%d" % slot)
             d_tiles[slot] = keep.tile([P, V], F32, name="d%d" % slot)
-            for entries, offsets in halves:
+            pieces = halves if slot == SLOT_ORDER[0] else [(slice(0, V), slice(0, V // 16))]
+            for entries, offsets in pieces:
                 nc.vector.tensor_copy(a_tiles[slot][:, entries], y_tiles[slot][:].indirect(la_sb[:, offsets]))
-            for entries, offsets in halves:
+            for entries, offsets in pieces:
                 nc.vector.tensor_tensor(
                     d_tiles[slot][:, entries], y_tiles[slot][:].indirect(lb_sb[:, offsets]), a_tiles[slot][:, entries], ALU.subtract
                 )

@@ -19,7 +19,6 @@ P = 128
 PACK = 4
 QUADS = 4
 CW = 128
-X_FIRST = 512
 SLOT_ORDER = (2, 0, 1, 3)
 
 
@@ -41,6 +40,7 @@ def tile_picked_mixscat_relu_po_kernel(
     nc = tc.nc
     with ExitStack() as ctx:
         keep = ctx.enter_context(tc.tile_pool(name="keep", bufs=1))
+        shared = ctx.enter_context(tc.tile_pool(name="shared", bufs=1))
         psum = ctx.enter_context(tc.psum_pool(name="psum", bufs=8))
 
         offs_sb = keep.tile([P, S // 16], U16, name="offs_sb")
@@ -50,7 +50,9 @@ def tile_picked_mixscat_relu_po_kernel(
         xs = keep.tile([P, T], U8, name="xs", align_bytes=64)
         chunks = H // CW
         chunk_cols = [slice(q * CW, (q + 1) * CW) for q in range(chunks)]
-        wa_raw = [keep.tile([P, PACK, CW], F32, name="wa_raw%d" % q, align_bytes=64) for q in range(chunks)]
+        wa_low = keep.tile([P, PACK, H // 2], F32, name="wa_low", align_bytes=64)
+        wa_high = shared.tile([P, PACK, H // 2], F32, name="wa_high", align_bytes=64, offset=0)
+        wa_raw = [(wa_low, wa_high)[q // 2][:, :, chunk_cols[q % 2]] for q in range(chunks)]
         gt_sb = keep.tile([P, PACK], F32, name="gt_sb", align_bytes=64)
         w1w = keep.tile([P, N], I32, name="w1w", align_bytes=64)
         w1s = keep.tile([P, N], U8, name="w1s", align_bytes=64)
@@ -59,13 +61,10 @@ def tile_picked_mixscat_relu_po_kernel(
         nc.vector.memset(w1s[:].bitcast(I32), 0)
         wa_rows = wa.rearrange("(p t) c -> p t c", t=PACK)
         nc.sync.dma_start(offs_sb[:], offs)
-        nc.sync.dma_start(out=wa_raw[0][:], in_=wa_rows[:, :, chunk_cols[0]])
-        x_rows = x_words[0].rearrange("p c t -> p (c t)").bitcast(I32)
-        nc.sync.dma_start(out=xw[:, :X_FIRST], in_=x_rows[:, :X_FIRST])
+        nc.sync.dma_start(out=wa_low[:], in_=wa_rows[:, :, : H // 2])
         load_scale_rows(nc.sync, xs, x_scales[0])
-        nc.sync.dma_start(out=xw[:, X_FIRST:], in_=x_rows[:, X_FIRST:])
-        for q in range(1, chunks):
-            nc.sync.dma_start(out=wa_raw[q][:], in_=wa_rows[:, :, chunk_cols[q]])
+        nc.sync.dma_start(out=xw[:], in_=x_words[0].rearrange("p c t -> p (c t)").bitcast(I32))
+        nc.sync.dma_start(out=wa_high[:], in_=wa_rows[:, :, H // 2 :])
         load_scale_rows(nc.sync, w1s, w1_scales[0])
         nc.sync.dma_start(out=w1w[:], in_=w1_words[0].rearrange("p c t -> p (c t)").bitcast(I32))
         nc.sync.dma_start(la_sb[:], la)
@@ -89,9 +88,10 @@ def tile_picked_mixscat_relu_po_kernel(
         for q in range(chunks):
             grouped = keep.tile([P, CW, PACK], BF16, name="wa_grouped%d" % q, align_bytes=64)
             cast = nc.vector.tensor_copy if q == chunks - 1 else nc.scalar.copy
-            cast(*interleave_views(grouped[:], wa_raw[q][:]))
+            cast(*interleave_views(grouped[:], wa_raw[q]))
             groups.append(grouped)
-        for grouped, cols in zip(groups, chunk_cols):
+        for q in (0, 1, 3, 2):
+            grouped, cols = groups[q], chunk_cols[q]
             nc.vector.quantize_mx(
                 out=wa_codes[:, cols].bitcast(FP8X4), scales=wa_scales[:, cols], in_=grouped[:].rearrange("p c t -> p (c t)")
             )
@@ -99,11 +99,11 @@ def tile_picked_mixscat_relu_po_kernel(
         def project(slot, y_sb, col_groups):
             rows = slice(slot * P, (slot + 1) * P)
             for col_list in col_groups:
-                first, last = col_list[0].start, col_list[-1].stop
-                bank = psum.tile([P, last - first], F32, name="bank", tag="bank")
+                begin, end = col_list[0].start, col_list[-1].stop
+                bank = psum.tile([P, end - begin], F32, name="bank", tag="bank")
                 for cols in col_list:
                     nc.tensor.matmul_mx(
-                        out=bank[:, cols.start - first : cols.stop - first],
+                        out=bank[:, cols.start - begin : cols.stop - begin],
                         lhsT=xw_dealt[:, rows].bitcast(FP8X4),
                         lhsT_scale=xs_dealt[:, rows],
                         rhs=wa_codes[:, cols].bitcast(FP8X4),
@@ -111,35 +111,38 @@ def tile_picked_mixscat_relu_po_kernel(
                         start=True,
                         stop=True,
                     )
-                nc.scalar.activation(y_sb[:, first:last], bank[:], ACT.Relu)
+                nc.scalar.activation(y_sb[:, begin:end], bank[:], ACT.Relu)
 
-        y_tiles = {}
-        for step, slot in enumerate(SLOT_ORDER):
-            if step == 0:
-                y_tiles[slot] = keep.tile([P, H], F32, name="wa_raw%d" % (chunks - 2), align_bytes=64)
-                project(slot, y_tiles[slot], [chunk_cols[:2], chunk_cols[2:3], chunk_cols[3:]])
-            else:
-                y_tiles[slot] = keep.tile([P, H], F32, name="y%d" % slot)
-                project(slot, y_tiles[slot], [[slice(0, H)]])
+        first, second, third, last = SLOT_ORDER
+        y_tiles = {
+            first: shared.tile([P, H], F32, name="y_first", align_bytes=64, offset=0),
+            second: shared.tile([P, H], F32, name="y_second", align_bytes=64, offset=4 * H),
+            third: keep.tile([P, H], F32, name="y_third"),
+            last: keep.tile([P, H], F32, name="y_last"),
+        }
+        low, high = slice(0, H // 2), slice(H // 2, H)
+        project(first, y_tiles[first], [chunk_cols[:2]])
+        project(second, y_tiles[second], [[low]])
+        project(first, y_tiles[first], [chunk_cols[3:], chunk_cols[2:3]])
+        project(second, y_tiles[second], [[high]])
+        for cols in (low, high):
+            project(third, y_tiles[third], [[cols]])
+            project(last, y_tiles[last], [[cols]])
 
         w1w_dealt = keep.tile([P, N], I32, name="w1w_dealt", align_bytes=64)
-        w1s_dealt = keep.tile([P, N], U8, name="wa_grouped%d" % (chunks - 1), align_bytes=64)
+        w1s_dealt = keep.tile([P, N], U8, name="wa_grouped%d" % (chunks - 2), align_bytes=64)
 
         z_grouped = [keep.tile([P, CW, PACK], BF16, name="z_grouped%d" % q, align_bytes=64) for q in range(chunks)]
 
         a_tiles, d_tiles, up_tiles, down_tiles, zs_tiles = {}, {}, {}, {}, {}
-        halves = [(slice(h * V // 2, (h + 1) * V // 2), slice(h * V // 32, (h + 1) * V // 32)) for h in range(2)]
 
-        def fetch(slot):
+        def fetch_a(slot):
             a_tiles[slot] = keep.tile([P, V], F32, name="a%d" % slot)
+            nc.vector.tensor_copy(a_tiles[slot][:], y_tiles[slot][:].indirect(la_sb[:]))
+
+        def fetch_d(slot):
             d_tiles[slot] = keep.tile([P, V], F32, name="d%d" % slot)
-            pieces = halves if slot == SLOT_ORDER[0] else [(slice(0, V), slice(0, V // 16))]
-            for entries, offsets in pieces:
-                nc.vector.tensor_copy(a_tiles[slot][:, entries], y_tiles[slot][:].indirect(la_sb[:, offsets]))
-            for entries, offsets in pieces:
-                nc.vector.tensor_tensor(
-                    d_tiles[slot][:, entries], y_tiles[slot][:].indirect(lb_sb[:, offsets]), a_tiles[slot][:, entries], ALU.subtract
-                )
+            nc.vector.tensor_tensor(d_tiles[slot][:], y_tiles[slot][:].indirect(lb_sb[:]), a_tiles[slot][:], ALU.subtract)
 
         def rise(slot):
             up_tiles[slot] = keep.tile([P, V], F32, name="up%d" % slot)
@@ -168,15 +171,17 @@ def tile_picked_mixscat_relu_po_kernel(
                 else:
                     nc.scalar.activation(z_grouped[q][:, :, slot], zs[:, cols], ACT.Copy, scale=gt_sb[:, slot : slot + 1])
 
-        for slot in SLOT_ORDER:
-            fetch(slot)
+        for pair in ((first, second), (third, last)):
+            for slot in pair:
+                fetch_a(slot)
+            for slot in pair:
+                fetch_d(slot)
         nc.vector.tensor_copy(
             w1w_dealt[:].rearrange("p (t m) -> p m t", t=PACK), w1w[:].rearrange("p (m t) -> p m t", t=PACK)
         )
         nc.vector.tensor_copy(
             w1s_dealt[:].rearrange("p (t m) -> p m t", t=PACK), w1s[:].rearrange("p (m t) -> p m t", t=PACK)
         )
-        first, second, third, last = SLOT_ORDER
         rise(first)
         rise(second)
         fall(first)

@@ -17,27 +17,54 @@ ACT = mybir.ActivationFunctionType
 
 P = 128
 PACK = 4
-QUADS = 4
+QUAD = 32
+LINE = 4
 CW = 128
+CHUNKS = H // CW
+CHUNK_COLS = [slice(q * CW, (q + 1) * CW) for q in range(CHUNKS)]
+HALF_COLS = [slice(0, H // 2), slice(H // 2, H)]
 SLOT_ORDER = (2, 0, 1, 3)
 
 
-def load_scale_rows(queue, plane, rows):
+def load_scale_rows(nc, plane, rows):
     for r in range(PACK):
-        queue.dma_start(out=plane[r:P:32, :].bitcast(I32), in_=rows[r : 4 * QUADS : 4, :].bitcast(I32))
+        nc.sync.dma_start(out=plane[r:P:QUAD, :].bitcast(I32), in_=rows[r::PACK, :].bitcast(I32))
 
 
-def interleave_views(grouped, planes):
-    return (
-        grouped.rearrange("p (c i) t -> p c t i", i=4),
-        planes.rearrange("p t (c i) -> p c t i", i=4),
+def deal_views(dealt, plain):
+    return dealt.rearrange("p (t m) -> p m t", t=PACK), plain.rearrange("p (m t) -> p m t", t=PACK)
+
+
+def interleave_views(grouped, slots):
+    return grouped.rearrange("p (c i) t -> p c t i", i=LINE), slots.rearrange("p t (c i) -> p c t i", i=LINE)
+
+
+def quantise(nc, codes, scales, grouped):
+    nc.vector.quantize_mx(out=codes.bitcast(FP8X4), scales=scales, in_=grouped.rearrange("p c t -> p (c t)"))
+
+
+def multiply(nc, out, left_codes, left_scales, right_codes, right_scales):
+    nc.tensor.matmul_mx(
+        out=out,
+        lhsT=left_codes.bitcast(FP8X4),
+        lhsT_scale=left_scales,
+        rhs=right_codes.bitcast(FP8X4),
+        rhs_scale=right_scales,
+        start=True,
+        stop=True,
     )
+
+
+def slot_cols(slot):
+    return slice(slot * P, (slot + 1) * P)
 
 
 def tile_picked_mixscat_relu_po_kernel(
     tc, x_words, x_scales, wa, gt, w1_words, w1_scales, offs, la, lb, out_0, out_1, out_2
 ):
     nc = tc.nc
+    first, second, third, last = SLOT_ORDER
+    low, high = HALF_COLS
     with ExitStack() as ctx:
         keep = ctx.enter_context(tc.tile_pool(name="keep", bufs=1))
         shared = ctx.enter_context(tc.tile_pool(name="shared", bufs=1))
@@ -48,92 +75,77 @@ def tile_picked_mixscat_relu_po_kernel(
         lb_sb = keep.tile([P, V // 16], U16, name="lb_sb")
         xw = keep.tile([P, T], I32, name="xw", align_bytes=64)
         xs = keep.tile([P, T], U8, name="xs", align_bytes=64)
-        chunks = H // CW
-        chunk_cols = [slice(q * CW, (q + 1) * CW) for q in range(chunks)]
         wa_low = keep.tile([P, PACK, H // 2], F32, name="wa_low", align_bytes=64)
         wa_high = shared.tile([P, PACK, H // 2], F32, name="wa_high", align_bytes=64, offset=0)
-        wa_raw = [(wa_low, wa_high)[q // 2][:, :, chunk_cols[q % 2]] for q in range(chunks)]
         gt_sb = keep.tile([P, PACK], F32, name="gt_sb", align_bytes=64)
         w1w = keep.tile([P, N], I32, name="w1w", align_bytes=64)
         w1s = keep.tile([P, N], U8, name="w1s", align_bytes=64)
 
         nc.vector.memset(xs[:].bitcast(I32), 0)
         nc.vector.memset(w1s[:].bitcast(I32), 0)
+
         wa_rows = wa.rearrange("(p t) c -> p t c", t=PACK)
         nc.sync.dma_start(offs_sb[:], offs)
-        nc.sync.dma_start(out=wa_low[:], in_=wa_rows[:, :, : H // 2])
-        load_scale_rows(nc.sync, xs, x_scales[0])
+        nc.sync.dma_start(out=wa_low[:], in_=wa_rows[:, :, low])
+        load_scale_rows(nc, xs, x_scales[0])
         nc.sync.dma_start(out=xw[:], in_=x_words[0].rearrange("p c t -> p (c t)").bitcast(I32))
-        nc.sync.dma_start(out=wa_high[:], in_=wa_rows[:, :, H // 2 :])
-        load_scale_rows(nc.sync, w1s, w1_scales[0])
+        nc.sync.dma_start(out=wa_high[:], in_=wa_rows[:, :, high])
+        load_scale_rows(nc, w1s, w1_scales[0])
         nc.sync.dma_start(out=w1w[:], in_=w1_words[0].rearrange("p c t -> p (c t)").bitcast(I32))
         nc.sync.dma_start(la_sb[:], la)
         nc.sync.dma_start(lb_sb[:], lb)
         nc.sync.dma_start(out=gt_sb[:], in_=gt.rearrange("(p t) o -> p (t o)", t=PACK))
 
         xs_picked = keep.tile([P, S], U8, name="xs_picked", align_bytes=64)
-        xs_dealt = keep.tile([P, S], U8, name="xs_dealt", align_bytes=64)
+        xs_even = keep.tile([P, S // 2], U8, name="xs_even", align_bytes=64)
         xw_dealt = keep.tile([P, S], I32, name="xw_dealt", align_bytes=64)
         nc.vector.tensor_copy(xs_picked[:], xs[:].indirect(offs_sb[:]))
-        nc.vector.tensor_copy(
-            xs_dealt[:].rearrange("p (t m) -> p m t", t=PACK), xs_picked[:].rearrange("p (m t) -> p m t", t=PACK)
-        )
+        xs_by_parity = xs_picked[:].rearrange("p (m u e) -> p e m u", u=2, e=2)
+        nc.vector.tensor_copy(xs_even[:].rearrange("p (u m) -> p m u", u=2), xs_by_parity[:, 0])
         nc.vector.tensor_copy(
             xw_dealt[:].bitcast(U32).rearrange("p (t m) -> p m t", t=PACK), xw[:].bitcast(U32).indirect(offs_sb[:])
         )
 
         wa_codes = keep.tile([P, H], I32, name="wa_codes", align_bytes=64)
         wa_scales = keep.tile([P, H], U8, name="wa_scales", align_bytes=64)
-        groups = []
-        for q in range(chunks):
-            grouped = keep.tile([P, CW, PACK], BF16, name="wa_grouped%d" % q, align_bytes=64)
-            cast = nc.vector.tensor_copy if q == chunks - 1 else nc.scalar.copy
-            cast(*interleave_views(grouped[:], wa_raw[q]))
-            groups.append(grouped)
-        for q in (0, 1, 3, 2):
-            grouped, cols = groups[q], chunk_cols[q]
-            nc.vector.quantize_mx(
-                out=wa_codes[:, cols].bitcast(FP8X4), scales=wa_scales[:, cols], in_=grouped[:].rearrange("p c t -> p (c t)")
-            )
+        wa_pieces = (
+            (nc.scalar.copy, wa_low[:], low, "wa_grouped_low"),
+            (nc.vector.tensor_copy, wa_high[:, :, CW:], CHUNK_COLS[3], "wa_grouped3"),
+            (nc.scalar.copy, wa_high[:, :, :CW], CHUNK_COLS[2], "wa_grouped2"),
+        )
+        for cast, piece, cols, tag in wa_pieces:
+            grouped = keep.tile([P, cols.stop - cols.start, PACK], BF16, name=tag, align_bytes=64)
+            cast(*interleave_views(grouped[:], piece))
+            quantise(nc, wa_codes[:, cols], wa_scales[:, cols], grouped[:])
 
-        def project(slot, y_sb, col_groups):
-            rows = slice(slot * P, (slot + 1) * P)
-            for col_list in col_groups:
-                begin, end = col_list[0].start, col_list[-1].stop
-                bank = psum.tile([P, end - begin], F32, name="bank", tag="bank")
-                for cols in col_list:
-                    nc.tensor.matmul_mx(
-                        out=bank[:, cols.start - begin : cols.stop - begin],
-                        lhsT=xw_dealt[:, rows].bitcast(FP8X4),
-                        lhsT_scale=xs_dealt[:, rows],
-                        rhs=wa_codes[:, cols].bitcast(FP8X4),
-                        rhs_scale=wa_scales[:, cols],
-                        start=True,
-                        stop=True,
-                    )
-                nc.scalar.activation(y_sb[:, begin:end], bank[:], ACT.Relu)
+        xs_odd = keep.tile([P, S // 2], U8, name="xs_odd", tag="wa_grouped3", align_bytes=64)
+        nc.vector.tensor_copy(xs_odd[:].rearrange("p (u m) -> p m u", u=2), xs_by_parity[:, 1])
 
-        first, second, third, last = SLOT_ORDER
         y_tiles = {
             first: shared.tile([P, H], F32, name="y_first", align_bytes=64, offset=0),
             second: shared.tile([P, H], F32, name="y_second", align_bytes=64, offset=4 * H),
             third: keep.tile([P, H], F32, name="y_third"),
             last: keep.tile([P, H], F32, name="y_last"),
         }
-        low, high = slice(0, H // 2), slice(H // 2, H)
-        project(first, y_tiles[first], [chunk_cols[:2]])
-        project(second, y_tiles[second], [[low]])
-        project(first, y_tiles[first], [chunk_cols[3:], chunk_cols[2:3]])
-        project(second, y_tiles[second], [[high]])
-        for cols in (low, high):
-            project(third, y_tiles[third], [[cols]])
-            project(last, y_tiles[last], [[cols]])
+
+        def project(slot, cols):
+            bank = psum.tile([P, cols.stop - cols.start], F32, name="bank", tag="bank")
+            slot_scales = (xs_even, xs_odd)[slot % 2][:, slot_cols(slot // 2)]
+            multiply(nc, bank[:], xw_dealt[:, slot_cols(slot)], slot_scales, wa_codes[:, cols], wa_scales[:, cols])
+            nc.scalar.activation(y_tiles[slot][:, cols], bank[:], ACT.Relu)
+
+        project(first, low)
+        project(second, low)
+        project(first, CHUNK_COLS[3])
+        project(first, CHUNK_COLS[2])
+        project(second, high)
+        for cols in HALF_COLS:
+            project(third, cols)
+            project(last, cols)
 
         w1w_dealt = keep.tile([P, N], I32, name="w1w_dealt", align_bytes=64)
-        w1s_dealt = keep.tile([P, N], U8, name="wa_grouped%d" % (chunks - 2), align_bytes=64)
-
-        z_grouped = [keep.tile([P, CW, PACK], BF16, name="z_grouped%d" % q, align_bytes=64) for q in range(chunks)]
-
+        w1s_dealt = keep.tile([P, N], U8, name="w1s_dealt", tag="wa_grouped2", align_bytes=64)
+        z_grouped = [keep.tile([P, CW, PACK], BF16, name="z_grouped%d" % q, align_bytes=64) for q in range(CHUNKS)]
         a_tiles, d_tiles, up_tiles, down_tiles, zs_tiles = {}, {}, {}, {}, {}
 
         def fetch_a(slot):
@@ -148,10 +160,9 @@ def tile_picked_mixscat_relu_po_kernel(
             up_tiles[slot] = keep.tile([P, V], F32, name="up%d" % slot)
             nc.scalar.activation(up_tiles[slot][:], d_tiles[slot][:], ACT.Relu)
 
-        def fall(slot):
+        def fall(slot, tag):
             drop = keep.tile([P, V], F32, name="drop%d" % slot)
-            tag = "zs%d" % SLOT_ORDER[0] if slot == SLOT_ORDER[-1] else "down%d" % slot
-            down_tiles[slot] = keep.tile([P, V], F32, name=tag)
+            down_tiles[slot] = keep.tile([P, V], F32, name="down%d" % slot, tag=tag)
             nc.scalar.activation(drop[:], d_tiles[slot][:], ACT.Relu, scale=-1.0)
             nc.scalar.activation(down_tiles[slot][:], drop[:], ACT.Copy, scale=-1.0)
 
@@ -163,41 +174,31 @@ def tile_picked_mixscat_relu_po_kernel(
             nc.vector.tensor_tensor(zs_tiles[slot][:].indirect(la_sb[:]), a_tiles[slot][:], down_tiles[slot][:], ALU.add)
 
         def weigh(slot):
-            zs = zs_tiles[slot]
-            for q in range(chunks):
-                cols = slice(q * CW, (q + 1) * CW)
-                if slot == SLOT_ORDER[-1] and q < chunks // 2:
-                    nc.vector.tensor_scalar(z_grouped[q][:, :, slot], zs[:, cols], gt_sb[:, slot : slot + 1], None, ALU.mult)
+            weight = gt_sb[:, slot : slot + 1]
+            for q in range(CHUNKS):
+                zs_chunk = zs_tiles[slot][:, CHUNK_COLS[q]]
+                if slot == last and q < CHUNKS // 2:
+                    nc.vector.tensor_scalar(z_grouped[q][:, :, slot], zs_chunk, weight, None, ALU.mult)
                 else:
-                    nc.scalar.activation(z_grouped[q][:, :, slot], zs[:, cols], ACT.Copy, scale=gt_sb[:, slot : slot + 1])
+                    nc.scalar.activation(z_grouped[q][:, :, slot], zs_chunk, ACT.Copy, scale=weight)
 
         for pair in ((first, second), (third, last)):
             for slot in pair:
                 fetch_a(slot)
             for slot in pair:
                 fetch_d(slot)
-        nc.vector.tensor_copy(
-            w1w_dealt[:].rearrange("p (t m) -> p m t", t=PACK), w1w[:].rearrange("p (m t) -> p m t", t=PACK)
-        )
-        nc.vector.tensor_copy(
-            w1s_dealt[:].rearrange("p (t m) -> p m t", t=PACK), w1s[:].rearrange("p (m t) -> p m t", t=PACK)
-        )
+        nc.vector.tensor_copy(*deal_views(w1w_dealt[:], w1w[:]))
+        nc.vector.tensor_copy(*deal_views(w1s_dealt[:], w1s[:]))
         rise(first)
-        rise(second)
-        fall(first)
-        rise(third)
-        fall(second)
-        rise(last)
-        fall(third)
+        for slot, following in zip(SLOT_ORDER, SLOT_ORDER[1:]):
+            rise(following)
+            fall(slot, "down%d" % slot)
         put_larger(first)
-        put_larger(second)
-        put_smaller(first)
-        put_larger(third)
-        put_smaller(second)
-        put_larger(last)
-        put_smaller(third)
+        for slot, following in zip(SLOT_ORDER, SLOT_ORDER[1:]):
+            put_larger(following)
+            put_smaller(slot)
         weigh(first)
-        fall(last)
+        fall(last, "zs%d" % first)
         put_smaller(last)
         for slot in SLOT_ORDER[1:]:
             weigh(slot)
@@ -208,37 +209,48 @@ def tile_picked_mixscat_relu_po_kernel(
         o_scales = keep.tile([P, H], U8, name="o_scales", align_bytes=64)
         out_rows = out_0.rearrange("(p t) c -> p t c", t=PACK)
         out_words = out_1[0].rearrange("p c t -> p (c t)").bitcast(I32)
-        for q in range(chunks):
-            cols = slice(q * CW, (q + 1) * CW)
-            nc.vector.quantize_mx(
-                out=z_codes[:, cols].bitcast(FP8X4), scales=z_scales[:, cols], in_=z_grouped[q][:].rearrange("p c t -> p (c t)")
-            )
-        for q in range(chunks):
-            cols = slice(q * CW, (q + 1) * CW)
-            o_sb = keep.tile([P, PACK, CW], F32, name="o_sb%d" % q, align_bytes=64)
+        for q in range(CHUNKS):
+            quantise(nc, z_codes[:, CHUNK_COLS[q]], z_scales[:, CHUNK_COLS[q]], z_grouped[q][:])
+        o_halves = [keep.tile([P, PACK, H // 2], F32, name="o_half%d" % h, align_bytes=64) for h in range(2)]
+
+        def mix(q, pair):
+            bank = psum.tile([P, 2, CW], F32, name="bank", tag="bank")
+            for place in range(2):
+                slot = 2 * pair + place
+                multiply(
+                    nc,
+                    bank[:, place, :],
+                    w1w_dealt[:, slot_cols(slot)],
+                    w1s_dealt[:, slot_cols(slot)],
+                    z_codes[:, CHUNK_COLS[q]],
+                    z_scales[:, CHUNK_COLS[q]],
+                )
+            nc.scalar.copy(o_halves[q // 2][:, 2 * pair : 2 * pair + 2, CHUNK_COLS[q % 2]], bank[:])
+
+        def store(h, pair):
+            places = slice(2 * pair, 2 * pair + 2)
+            nc.sync.dma_start(out=out_rows[:, places, HALF_COLS[h]], in_=o_halves[h][:, places, :])
+
+        def quantise_out(q):
             o_grouped = keep.tile([P, CW, PACK], BF16, name="o_grouped%d" % q, align_bytes=64)
-            for pair in range(PACK // 2):
-                bank = psum.tile([P, 2, CW], F32, name="bank", tag="bank")
-                for place in range(2):
-                    rows = slice((2 * pair + place) * P, (2 * pair + place + 1) * P)
-                    nc.tensor.matmul_mx(
-                        out=bank[:, place, :],
-                        lhsT=w1w_dealt[:, rows].bitcast(FP8X4),
-                        lhsT_scale=w1s_dealt[:, rows],
-                        rhs=z_codes[:, cols].bitcast(FP8X4),
-                        rhs_scale=z_scales[:, cols],
-                        start=True,
-                        stop=True,
-                    )
-                nc.scalar.copy(o_sb[:, 2 * pair : 2 * pair + 2, :], bank[:])
-            nc.sync.dma_start(out=out_rows[:, :, cols], in_=o_sb[:])
-            nc.vector.tensor_copy(*interleave_views(o_grouped[:], o_sb[:]))
-            nc.vector.quantize_mx(
-                out=o_codes[:, cols].bitcast(FP8X4), scales=o_scales[:, cols], in_=o_grouped[:].rearrange("p c t -> p (c t)")
-            )
-            if q % 2 == 1:
-                half = slice((q - 1) * CW, (q + 1) * CW)
-                nc.sync.dma_start(out=out_words[:, half], in_=o_codes[:, half])
+            nc.vector.tensor_copy(*interleave_views(o_grouped[:], o_halves[q // 2][:, :, CHUNK_COLS[q % 2]]))
+            quantise(nc, o_codes[:, CHUNK_COLS[q]], o_scales[:, CHUNK_COLS[q]], o_grouped[:])
+
+        for pair in range(2):
+            mix(0, pair)
+            mix(1, pair)
+            store(0, pair)
+        quantise_out(0)
+        quantise_out(1)
+        nc.sync.dma_start(out=out_words[:, low], in_=o_codes[:, low])
+        for pair in range(2):
+            mix(2, pair)
+        quantise_out(2)
+        for pair in range(2):
+            mix(3, pair)
+            store(1, pair)
+        quantise_out(3)
+        nc.sync.dma_start(out=out_words[:, high], in_=o_codes[:, high])
         for r in range(PACK):
             queue = nc.scalar if r % 2 == 0 else nc.sync
-            queue.dma_start(out=out_2[0, r : 4 * QUADS : 4, :].bitcast(I32), in_=o_scales[r:P:32, :].bitcast(I32))
+            queue.dma_start(out=out_2[0, r::PACK, :].bitcast(I32), in_=o_scales[r:P:QUAD, :].bitcast(I32))

@@ -18,6 +18,7 @@ ACT = mybir.ActivationFunctionType
 P = 128
 PACK = 4
 QUAD = 32
+BLOCK = 8
 LINE = 4
 CW = 128
 CHUNKS = H // CW
@@ -29,6 +30,10 @@ SLOT_ORDER = (2, 0, 1, 3)
 def load_scale_rows(nc, plane, rows):
     for r in range(PACK):
         nc.sync.dma_start(out=plane[r:P:QUAD, :].bitcast(I32), in_=rows[r::PACK, :].bitcast(I32))
+
+
+def deal_bytes(nc, dealt, plain):
+    nc.vector.tensor_copy(dealt.rearrange("p (t m) -> p t m", t=PACK), plain.rearrange("p (m t) -> p t m", t=PACK))
 
 
 def deal_views(dealt, plain):
@@ -88,20 +93,21 @@ def tile_picked_mixscat_relu_po_kernel(
         nc.sync.dma_start(offs_sb[:], offs)
         nc.sync.dma_start(out=wa_low[:], in_=wa_rows[:, :, low])
         load_scale_rows(nc, xs, x_scales[0])
+        nc.sync.dma_start(out=w1s[0:P:BLOCK, :].bitcast(I32), in_=w1_scales[0].bitcast(I32))
         nc.sync.dma_start(out=xw[:], in_=x_words[0].rearrange("p c t -> p (c t)").bitcast(I32))
         nc.sync.dma_start(out=wa_high[:], in_=wa_rows[:, :, high])
-        load_scale_rows(nc, w1s, w1_scales[0])
         nc.sync.dma_start(out=w1w[:], in_=w1_words[0].rearrange("p c t -> p (c t)").bitcast(I32))
         nc.sync.dma_start(la_sb[:], la)
         nc.sync.dma_start(lb_sb[:], lb)
         nc.sync.dma_start(out=gt_sb[:], in_=gt.rearrange("(p t) o -> p (t o)", t=PACK))
 
         xs_picked = keep.tile([P, S], U8, name="xs_picked", align_bytes=64)
-        xs_even = keep.tile([P, S // 2], U8, name="xs_even", align_bytes=64)
+        xs_dealt = keep.tile([P, S], U8, name="xs_dealt", align_bytes=64)
+        w1s_dealt = keep.tile([P, N], U8, name="w1s_dealt", align_bytes=64)
         xw_dealt = keep.tile([P, S], I32, name="xw_dealt", align_bytes=64)
         nc.vector.tensor_copy(xs_picked[:], xs[:].indirect(offs_sb[:]))
-        xs_by_parity = xs_picked[:].rearrange("p (m u e) -> p e m u", u=2, e=2)
-        nc.vector.tensor_copy(xs_even[:].rearrange("p (u m) -> p m u", u=2), xs_by_parity[:, 0])
+        deal_bytes(nc, w1s_dealt[:], w1s[:])
+        deal_bytes(nc, xs_dealt[:], xs_picked[:])
         nc.vector.tensor_copy(
             xw_dealt[:].bitcast(U32).rearrange("p (t m) -> p m t", t=PACK), xw[:].bitcast(U32).indirect(offs_sb[:])
         )
@@ -110,16 +116,18 @@ def tile_picked_mixscat_relu_po_kernel(
         wa_scales = keep.tile([P, H], U8, name="wa_scales", align_bytes=64)
         wa_pieces = (
             (nc.scalar.copy, wa_low[:], low, "wa_grouped_low"),
-            (nc.vector.tensor_copy, wa_high[:, :, CW:], CHUNK_COLS[3], "wa_grouped3"),
+            (nc.vector.tensor_copy, wa_high[:, :, CW : CW + CW // 2], slice(3 * CW, 3 * CW + CW // 2), "wa_grouped3a"),
+            (nc.vector.tensor_copy, wa_high[:, :, CW + CW // 2 :], slice(3 * CW + CW // 2, H), "wa_grouped3b"),
             (nc.scalar.copy, wa_high[:, :, :CW], CHUNK_COLS[2], "wa_grouped2"),
         )
+        rounded = []
         for cast, piece, cols, tag in wa_pieces:
             grouped = keep.tile([P, cols.stop - cols.start, PACK], BF16, name=tag, align_bytes=64)
             cast(*interleave_views(grouped[:], piece))
+            rounded.append((cols, grouped))
+        for cols, grouped in rounded:
             quantise(nc, wa_codes[:, cols], wa_scales[:, cols], grouped[:])
 
-        xs_odd = keep.tile([P, S // 2], U8, name="xs_odd", tag="wa_grouped3", align_bytes=64)
-        nc.vector.tensor_copy(xs_odd[:].rearrange("p (u m) -> p m u", u=2), xs_by_parity[:, 1])
 
         y_tiles = {
             first: shared.tile([P, H], F32, name="y_first", align_bytes=64, offset=0),
@@ -130,9 +138,12 @@ def tile_picked_mixscat_relu_po_kernel(
 
         def project(slot, cols):
             bank = psum.tile([P, cols.stop - cols.start], F32, name="bank", tag="bank")
-            slot_scales = (xs_even, xs_odd)[slot % 2][:, slot_cols(slot // 2)]
+            slot_scales = xs_dealt[:, slot_cols(slot)]
             multiply(nc, bank[:], xw_dealt[:, slot_cols(slot)], slot_scales, wa_codes[:, cols], wa_scales[:, cols])
-            nc.scalar.activation(y_tiles[slot][:, cols], bank[:], ACT.Relu)
+            if slot == second and cols == low:
+                nc.vector.tensor_scalar(y_tiles[slot][:, cols], bank[:], 0.0, None, ALU.max)
+            else:
+                nc.scalar.activation(y_tiles[slot][:, cols], bank[:], ACT.Relu)
 
         project(first, low)
         project(second, low)
@@ -143,8 +154,6 @@ def tile_picked_mixscat_relu_po_kernel(
             project(third, cols)
             project(last, cols)
 
-        w1w_dealt = keep.tile([P, N], I32, name="w1w_dealt", align_bytes=64)
-        w1s_dealt = keep.tile([P, N], U8, name="w1s_dealt", tag="wa_grouped2", align_bytes=64)
         z_grouped = [keep.tile([P, CW, PACK], BF16, name="z_grouped%d" % q, align_bytes=64) for q in range(CHUNKS)]
         a_tiles, d_tiles, up_tiles, down_tiles, zs_tiles = {}, {}, {}, {}, {}
 
@@ -161,7 +170,7 @@ def tile_picked_mixscat_relu_po_kernel(
             nc.scalar.activation(up_tiles[slot][:], d_tiles[slot][:], ACT.Relu)
 
         def fall(slot, tag):
-            drop = keep.tile([P, V], F32, name="drop%d" % slot)
+            drop = keep.tile([P, V], F32, name="drop%d" % slot, align_bytes=64)
             down_tiles[slot] = keep.tile([P, V], F32, name="down%d" % slot, tag=tag)
             nc.scalar.activation(drop[:], d_tiles[slot][:], ACT.Relu, scale=-1.0)
             nc.scalar.activation(down_tiles[slot][:], drop[:], ACT.Copy, scale=-1.0)
@@ -187,8 +196,10 @@ def tile_picked_mixscat_relu_po_kernel(
                 fetch_a(slot)
             for slot in pair:
                 fetch_d(slot)
-        nc.vector.tensor_copy(*deal_views(w1w_dealt[:], w1w[:]))
-        nc.vector.tensor_copy(*deal_views(w1s_dealt[:], w1s[:]))
+        for r in range(1, PACK):
+            nc.sync.dma_start(
+                out=w1s_dealt[r:P:QUAD, :].bitcast(I32), in_=w1s_dealt[BLOCK * r : P : QUAD, :].bitcast(I32)
+            )
         rise(first)
         for slot, following in zip(SLOT_ORDER, SLOT_ORDER[1:]):
             rise(following)
@@ -200,6 +211,8 @@ def tile_picked_mixscat_relu_po_kernel(
         weigh(first)
         fall(last, "zs%d" % first)
         put_smaller(last)
+        w1w_dealt = keep.tile([P, N], I32, name="w1w_dealt", tag="drop%d" % last, align_bytes=64)
+        nc.vector.tensor_copy(*deal_views(w1w_dealt[:], w1w[:]))
         for slot in SLOT_ORDER[1:]:
             weigh(slot)
 

@@ -114,10 +114,11 @@ def tile_picked_mixscat_relu_po_kernel(
 
         wa_codes = keep.tile([P, H], I32, name="wa_codes", align_bytes=64)
         wa_scales = keep.tile([P, H], U8, name="wa_scales", align_bytes=64)
+        half_chunk = CW // 2
         wa_pieces = (
             (nc.scalar.copy, wa_low[:], low, "wa_grouped_low"),
-            (nc.vector.tensor_copy, wa_high[:, :, CW : CW + CW // 2], slice(3 * CW, 3 * CW + CW // 2), "wa_grouped3a"),
-            (nc.vector.tensor_copy, wa_high[:, :, CW + CW // 2 :], slice(3 * CW + CW // 2, H), "wa_grouped3b"),
+            (nc.vector.tensor_copy, wa_high[:, :, CW : CW + half_chunk], slice(H - CW, H - half_chunk), "wa_grouped3a"),
+            (nc.vector.tensor_copy, wa_high[:, :, CW + half_chunk :], slice(H - half_chunk, H), "wa_grouped3b"),
             (nc.scalar.copy, wa_high[:, :, :CW], CHUNK_COLS[2], "wa_grouped2"),
         )
         rounded = []
@@ -127,7 +128,6 @@ def tile_picked_mixscat_relu_po_kernel(
             rounded.append((cols, grouped))
         for cols, grouped in rounded:
             quantise(nc, wa_codes[:, cols], wa_scales[:, cols], grouped[:])
-
 
         y_tiles = {
             first: shared.tile([P, H], F32, name="y_first", align_bytes=64, offset=0),
@@ -170,7 +170,7 @@ def tile_picked_mixscat_relu_po_kernel(
             nc.scalar.activation(up_tiles[slot][:], d_tiles[slot][:], ACT.Relu)
 
         def fall(slot, tag):
-            drop = keep.tile([P, V], F32, name="drop%d" % slot, align_bytes=64)
+            drop = keep.tile([P, V], F32, name="drop%d" % slot)
             down_tiles[slot] = keep.tile([P, V], F32, name="down%d" % slot, tag=tag)
             nc.scalar.activation(drop[:], d_tiles[slot][:], ACT.Relu, scale=-1.0)
             nc.scalar.activation(down_tiles[slot][:], drop[:], ACT.Copy, scale=-1.0)
@@ -196,6 +196,8 @@ def tile_picked_mixscat_relu_po_kernel(
                 fetch_a(slot)
             for slot in pair:
                 fetch_d(slot)
+        w1w_dealt = keep.tile([P, N], I32, name="w1w_dealt", tag="wa_grouped2", align_bytes=64)
+        nc.vector.tensor_copy(*deal_views(w1w_dealt[:], w1w[:]))
         for r in range(1, PACK):
             nc.sync.dma_start(
                 out=w1s_dealt[r:P:QUAD, :].bitcast(I32), in_=w1s_dealt[BLOCK * r : P : QUAD, :].bitcast(I32)
@@ -211,8 +213,6 @@ def tile_picked_mixscat_relu_po_kernel(
         weigh(first)
         fall(last, "zs%d" % first)
         put_smaller(last)
-        w1w_dealt = keep.tile([P, N], I32, name="w1w_dealt", tag="drop%d" % last, align_bytes=64)
-        nc.vector.tensor_copy(*deal_views(w1w_dealt[:], w1w[:]))
         for slot in SLOT_ORDER[1:]:
             weigh(slot)
 
@@ -255,7 +255,6 @@ def tile_picked_mixscat_relu_po_kernel(
             store(0, pair)
         quantise_out(0)
         quantise_out(1)
-        nc.sync.dma_start(out=out_words[:, low], in_=o_codes[:, low])
         for pair in range(2):
             mix(2, pair)
         quantise_out(2)
@@ -263,7 +262,7 @@ def tile_picked_mixscat_relu_po_kernel(
             mix(3, pair)
             store(1, pair)
         quantise_out(3)
-        nc.sync.dma_start(out=out_words[:, high], in_=o_codes[:, high])
+        nc.sync.dma_start(out=out_words, in_=o_codes[:])
         for r in range(PACK):
             queue = nc.scalar if r % 2 == 0 else nc.sync
             queue.dma_start(out=out_2[0, r::PACK, :].bitcast(I32), in_=o_scales[r:P:QUAD, :].bitcast(I32))

@@ -145,42 +145,55 @@ def tile_picked_mixscat_relu_po_kernel(
             else:
                 nc.scalar.activation(y_tiles[slot][:, cols], bank[:], ACT.Relu)
 
-        project(first, low)
-        project(second, low)
-        project(first, CHUNK_COLS[3])
-        project(first, CHUNK_COLS[2])
-        project(second, high)
-        for cols in HALF_COLS:
-            project(third, cols)
-            project(last, cols)
+        z_base = 2 * 4 * H
+        z_grouped = [
+            shared.tile([P, CW, PACK], BF16, name="z_grouped%d" % q, align_bytes=64, offset=z_base + q * 2 * PACK * CW)
+            for q in range(CHUNKS)
+        ]
+        a_tiles, b_tiles, larger, smaller, zs_tiles = {}, {}, {}, {}, {}
 
-        z_grouped = [keep.tile([P, CW, PACK], BF16, name="z_grouped%d" % q, align_bytes=64) for q in range(CHUNKS)]
-        a_tiles, d_tiles, up_tiles, down_tiles, zs_tiles = {}, {}, {}, {}, {}
-
-        def fetch_a(slot):
+        def fetch(slot):
             a_tiles[slot] = keep.tile([P, V], F32, name="a%d" % slot)
-            nc.vector.tensor_copy(a_tiles[slot][:], y_tiles[slot][:].indirect(la_sb[:]))
+            b_tiles[slot] = keep.tile([P, V], F32, name="b%d" % slot)
+            nc.scalar.activation(a_tiles[slot][:], y_tiles[slot][:].indirect(la_sb[:]), ACT.Copy)
+            if slot == first:
+                nc.vector.tensor_copy(b_tiles[slot][:], y_tiles[slot][:].indirect(lb_sb[:]))
+            else:
+                nc.scalar.activation(b_tiles[slot][:], y_tiles[slot][:].indirect(lb_sb[:]), ACT.Copy)
 
-        def fetch_d(slot):
-            d_tiles[slot] = keep.tile([P, V], F32, name="d%d" % slot)
-            nc.vector.tensor_tensor(d_tiles[slot][:], y_tiles[slot][:].indirect(lb_sb[:]), a_tiles[slot][:], ALU.subtract)
+        def take_larger(slot):
+            larger[slot] = keep.tile([P, V], F32, name="larger%d" % slot)
+            nc.vector.tensor_tensor(larger[slot][:], a_tiles[slot][:], b_tiles[slot][:], ALU.max)
 
-        def rise(slot):
+        def take_smaller(slot, pool, **place):
+            smaller[slot] = pool.tile([P, V], F32, name="smaller%d" % slot, **place)
+            nc.vector.tensor_tensor(smaller[slot][:], a_tiles[slot][:], b_tiles[slot][:], ALU.min)
+
+        up_tiles = {}
+
+        def add_larger(slot):
+            if slot == last:
+                wide = shared.tile([P, CHUNKS * V], F32, name="gap_wide", align_bytes=64, offset=z_base)
+                gap = wide[:, :V]
+            else:
+                own = keep.tile([P, V], F32, name="gap%d" % slot)
+                gap = own[:]
             up_tiles[slot] = keep.tile([P, V], F32, name="up%d" % slot)
-            nc.scalar.activation(up_tiles[slot][:], d_tiles[slot][:], ACT.Relu)
+            larger[slot] = keep.tile([P, V], F32, name="larger%d" % slot)
+            nc.gpsimd.tensor_tensor(gap, b_tiles[slot][:], a_tiles[slot][:], ALU.subtract)
+            nc.scalar.activation(up_tiles[slot][:], gap, ACT.Relu)
+            nc.gpsimd.tensor_tensor(larger[slot][:], a_tiles[slot][:], up_tiles[slot][:], ALU.add)
 
-        def fall(slot, tag):
-            drop = keep.tile([P, V], F32, name="drop%d" % slot)
-            down_tiles[slot] = keep.tile([P, V], F32, name="down%d" % slot, tag=tag)
-            nc.scalar.activation(drop[:], d_tiles[slot][:], ACT.Relu, scale=-1.0)
-            nc.scalar.activation(down_tiles[slot][:], drop[:], ACT.Copy, scale=-1.0)
+        def add_smaller(slot, tag):
+            smaller[slot] = keep.tile([P, V], F32, name="smaller%d" % slot, tag=tag)
+            nc.gpsimd.tensor_tensor(smaller[slot][:], b_tiles[slot][:], up_tiles[slot][:], ALU.subtract)
 
         def put_larger(slot):
             zs_tiles[slot] = keep.tile([P, H], F32, name="zs%d" % slot)
-            nc.vector.tensor_tensor(zs_tiles[slot][:].indirect(lb_sb[:]), a_tiles[slot][:], up_tiles[slot][:], ALU.add)
+            nc.vector.tensor_copy(zs_tiles[slot][:].indirect(lb_sb[:]), larger[slot][:])
 
         def put_smaller(slot):
-            nc.vector.tensor_tensor(zs_tiles[slot][:].indirect(la_sb[:]), a_tiles[slot][:], down_tiles[slot][:], ALU.add)
+            nc.vector.tensor_copy(zs_tiles[slot][:].indirect(la_sb[:]), smaller[slot][:])
 
         def weigh(slot):
             weight = gt_sb[:, slot : slot + 1]
@@ -191,27 +204,38 @@ def tile_picked_mixscat_relu_po_kernel(
                 else:
                     nc.scalar.activation(z_grouped[q][:, :, slot], zs_chunk, ACT.Copy, scale=weight)
 
-        for pair in ((first, second), (third, last)):
-            for slot in pair:
-                fetch_a(slot)
-            for slot in pair:
-                fetch_d(slot)
+        project(first, low)
+        project(second, low)
+        project(first, CHUNK_COLS[3])
+        project(first, CHUNK_COLS[2])
+        fetch(first)
+        project(second, high)
+        fetch(second)
+        add_larger(second)
+        for slot in (third, last):
+            for cols in HALF_COLS:
+                project(slot, cols)
+            fetch(slot)
+            add_larger(slot)
         w1w_dealt = keep.tile([P, N], I32, name="w1w_dealt", tag="wa_grouped2", align_bytes=64)
         nc.vector.tensor_copy(*deal_views(w1w_dealt[:], w1w[:]))
         for r in range(1, PACK):
             nc.sync.dma_start(
                 out=w1s_dealt[r:P:QUAD, :].bitcast(I32), in_=w1s_dealt[BLOCK * r : P : QUAD, :].bitcast(I32)
             )
-        rise(first)
-        for slot, following in zip(SLOT_ORDER, SLOT_ORDER[1:]):
-            rise(following)
-            fall(slot, "down%d" % slot)
+        take_larger(first)
+        take_smaller(first, keep)
         put_larger(first)
-        for slot, following in zip(SLOT_ORDER, SLOT_ORDER[1:]):
-            put_larger(following)
-            put_smaller(slot)
+        put_smaller(first)
+        add_smaller(second, "a%d" % third)
+        add_smaller(third, "a%d" % last)
         weigh(first)
-        fall(last, "zs%d" % first)
+        add_smaller(last, "zs%d" % first)
+        put_larger(second)
+        put_larger(third)
+        put_smaller(second)
+        put_larger(last)
+        put_smaller(third)
         put_smaller(last)
         for slot in SLOT_ORDER[1:]:
             weigh(slot)

@@ -32,10 +32,6 @@ def load_scale_rows(nc, plane, rows):
         nc.sync.dma_start(out=plane[r:P:QUAD, :].bitcast(I32), in_=rows[r::PACK, :].bitcast(I32))
 
 
-def deal_bytes(nc, dealt, plain):
-    nc.vector.tensor_copy(dealt.rearrange("p (t m) -> p t m", t=PACK), plain.rearrange("p (m t) -> p t m", t=PACK))
-
-
 def deal_views(dealt, plain):
     return dealt.rearrange("p (t m) -> p m t", t=PACK), plain.rearrange("p (m t) -> p m t", t=PACK)
 
@@ -87,27 +83,24 @@ def tile_picked_mixscat_relu_po_kernel(
         w1s = keep.tile([P, N], U8, name="w1s", align_bytes=64)
 
         nc.vector.memset(xs[:].bitcast(I32), 0)
-        nc.vector.memset(w1s[:].bitcast(I32), 0)
+        nc.gpsimd.memset(w1s[:].bitcast(I32), 0)
 
         wa_rows = wa.rearrange("(p t) c -> p t c", t=PACK)
         nc.sync.dma_start(offs_sb[:], offs)
+        x_rows = x_words[0].rearrange("p c t -> p (c t)").bitcast(I32)
         nc.sync.dma_start(out=wa_low[:], in_=wa_rows[:, :, low])
         load_scale_rows(nc, xs, x_scales[0])
-        nc.sync.dma_start(out=w1s[0:P:BLOCK, :].bitcast(I32), in_=w1_scales[0].bitcast(I32))
-        nc.sync.dma_start(out=xw[:], in_=x_words[0].rearrange("p c t -> p (c t)").bitcast(I32))
+        nc.sync.dma_start(out=xw[:], in_=x_rows)
         nc.sync.dma_start(out=wa_high[:], in_=wa_rows[:, :, high])
-        nc.sync.dma_start(out=w1w[:], in_=w1_words[0].rearrange("p c t -> p (c t)").bitcast(I32))
         nc.sync.dma_start(la_sb[:], la)
         nc.sync.dma_start(lb_sb[:], lb)
         nc.sync.dma_start(out=gt_sb[:], in_=gt.rearrange("(p t) o -> p (t o)", t=PACK))
+        nc.sync.dma_start(out=w1w[:], in_=w1_words[0].rearrange("p c t -> p (c t)").bitcast(I32))
+        load_scale_rows(nc, w1s, w1_scales[0])
 
-        xs_picked = keep.tile([P, S], U8, name="xs_picked", align_bytes=64)
         xs_dealt = keep.tile([P, S], U8, name="xs_dealt", align_bytes=64)
-        w1s_dealt = keep.tile([P, N], U8, name="w1s_dealt", align_bytes=64)
         xw_dealt = keep.tile([P, S], I32, name="xw_dealt", align_bytes=64)
-        nc.vector.tensor_copy(xs_picked[:], xs[:].indirect(offs_sb[:]))
-        deal_bytes(nc, w1s_dealt[:], w1s[:])
-        deal_bytes(nc, xs_dealt[:], xs_picked[:])
+        nc.vector.tensor_copy(xs_dealt[:].rearrange("p (t m) -> p m t", t=PACK), xs[:].indirect(offs_sb[:]))
         nc.vector.tensor_copy(
             xw_dealt[:].bitcast(U32).rearrange("p (t m) -> p m t", t=PACK), xw[:].bitcast(U32).indirect(offs_sb[:])
         )
@@ -121,13 +114,14 @@ def tile_picked_mixscat_relu_po_kernel(
             (nc.vector.tensor_copy, wa_high[:, :, CW + half_chunk :], slice(H - half_chunk, H), "wa_grouped3b"),
             (nc.scalar.copy, wa_high[:, :, :CW], CHUNK_COLS[2], "wa_grouped2"),
         )
-        rounded = []
-        for cast, piece, cols, tag in wa_pieces:
-            grouped = keep.tile([P, cols.stop - cols.start, PACK], BF16, name=tag, align_bytes=64)
-            cast(*interleave_views(grouped[:], piece))
-            rounded.append((cols, grouped))
-        for cols, grouped in rounded:
-            quantise(nc, wa_codes[:, cols], wa_scales[:, cols], grouped[:])
+        for pieces in (wa_pieces[:1], wa_pieces[1:]):
+            rounded = []
+            for cast, piece, cols, tag in pieces:
+                grouped = keep.tile([P, cols.stop - cols.start, PACK], BF16, name=tag, align_bytes=64)
+                cast(*interleave_views(grouped[:], piece))
+                rounded.append((cols, grouped))
+            for cols, grouped in rounded:
+                quantise(nc, wa_codes[:, cols], wa_scales[:, cols], grouped[:])
 
         y_tiles = {
             first: shared.tile([P, H], F32, name="y_first", align_bytes=64, offset=0),
@@ -154,7 +148,7 @@ def tile_picked_mixscat_relu_po_kernel(
 
         def fetch(slot):
             a_tiles[slot] = keep.tile([P, V], F32, name="a%d" % slot)
-            b_tiles[slot] = keep.tile([P, V], F32, name="b%d" % slot)
+            b_tiles[slot] = keep.tile([P, V], F32, align_bytes=64, name="b%d" % slot)
             nc.scalar.activation(a_tiles[slot][:], y_tiles[slot][:].indirect(la_sb[:]), ACT.Copy)
             if slot == first:
                 nc.vector.tensor_copy(b_tiles[slot][:], y_tiles[slot][:].indirect(lb_sb[:]))
@@ -176,9 +170,9 @@ def tile_picked_mixscat_relu_po_kernel(
                 wide = shared.tile([P, CHUNKS * V], F32, name="gap_wide", align_bytes=64, offset=z_base)
                 gap = wide[:, :V]
             else:
-                own = keep.tile([P, V], F32, name="gap%d" % slot)
+                own = keep.tile([P, V], F32, name="gap%d" % slot, tag="larger%d" % first)
                 gap = own[:]
-            up_tiles[slot] = keep.tile([P, V], F32, name="up%d" % slot)
+            up_tiles[slot] = keep.tile([P, V], F32, align_bytes=64, name="up%d" % slot)
             larger[slot] = keep.tile([P, V], F32, name="larger%d" % slot)
             nc.gpsimd.tensor_tensor(gap, b_tiles[slot][:], a_tiles[slot][:], ALU.subtract)
             nc.scalar.activation(up_tiles[slot][:], gap, ACT.Relu)
@@ -211,27 +205,30 @@ def tile_picked_mixscat_relu_po_kernel(
         fetch(first)
         project(second, high)
         fetch(second)
-        add_larger(second)
+        take_larger(first)
+        take_smaller(first, keep)
+        put_larger(first)
+        take_larger(second)
+        put_smaller(first)
+        put_larger(second)
+        up_tiles[second] = keep.tile([P, V], F32, align_bytes=64, name="up%d" % second)
+        nc.gpsimd.tensor_tensor(up_tiles[second][:], larger[second][:], a_tiles[second][:], ALU.subtract)
         for slot in (third, last):
             for cols in HALF_COLS:
                 project(slot, cols)
             fetch(slot)
             add_larger(slot)
-        w1w_dealt = keep.tile([P, N], I32, name="w1w_dealt", tag="wa_grouped2", align_bytes=64)
-        nc.vector.tensor_copy(*deal_views(w1w_dealt[:], w1w[:]))
-        for r in range(1, PACK):
-            nc.sync.dma_start(
-                out=w1s_dealt[r:P:QUAD, :].bitcast(I32), in_=w1s_dealt[BLOCK * r : P : QUAD, :].bitcast(I32)
-            )
-        take_larger(first)
-        take_smaller(first, keep)
-        put_larger(first)
-        put_smaller(first)
         add_smaller(second, "a%d" % third)
         add_smaller(third, "a%d" % last)
         weigh(first)
         add_smaller(last, "zs%d" % first)
-        put_larger(second)
+        w1w_dealt = keep.tile([P, N], I32, name="w1w_dealt", tag="b%d" % third, align_bytes=64)
+        dealt_view, plain_view = deal_views(w1w_dealt[:].bitcast(U32), w1w[:].bitcast(U32))
+        nc.scalar.copy(dealt_view, plain_view)
+        w1s_dealt = keep.tile([P, N], U8, name="w1s_dealt", tag="up%d" % last, align_bytes=64)
+        nc.gpsimd.tensor_copy(
+            w1s_dealt[:].rearrange("p (t m) -> p t m", t=PACK), w1s[:].rearrange("p (m t) -> p t m", t=PACK)
+        )
         put_larger(third)
         put_smaller(second)
         put_larger(last)

@@ -69,6 +69,7 @@ def tile_picked_mixscat_relu_po_kernel(
     with ExitStack() as ctx:
         keep = ctx.enter_context(tc.tile_pool(name="keep", bufs=1))
         shared = ctx.enter_context(tc.tile_pool(name="shared", bufs=1))
+        pair = ctx.enter_context(tc.tile_pool(name="pair", bufs=1))
         psum = ctx.enter_context(tc.psum_pool(name="psum", bufs=8))
 
         offs_sb = keep.tile([P, S // 16], U16, name="offs_sb")
@@ -78,29 +79,35 @@ def tile_picked_mixscat_relu_po_kernel(
         xs = keep.tile([P, T], U8, name="xs", align_bytes=64)
         wa_low = keep.tile([P, PACK, H // 2], F32, name="wa_low", align_bytes=64)
         wa_high = shared.tile([P, PACK, H // 2], F32, name="wa_high", align_bytes=64, offset=0)
-        gt_sb = keep.tile([P, PACK], F32, name="gt_sb", align_bytes=64)
-        w1w = keep.tile([P, N], I32, name="w1w", align_bytes=64)
-        w1s = keep.tile([P, N], U8, name="w1s", align_bytes=64)
+        late = ctx.enter_context(tc.tile_pool(name="late", bufs=1))
+        picked_at = 4 * N - 64
+        xs_picked = late.tile([P, S], U8, name="xs_picked", align_bytes=64, offset=picked_at)
+        xs_dealt = keep.tile([P, S], U8, name="xs_dealt", align_bytes=64)
 
         nc.vector.memset(xs[:].bitcast(I32), 0)
-        nc.gpsimd.memset(w1s[:].bitcast(I32), 0)
+        nc.gpsimd.memset(xs_dealt[:].bitcast(I32), 0)
 
         wa_rows = wa.rearrange("(p t) c -> p t c", t=PACK)
         nc.sync.dma_start(offs_sb[:], offs)
         x_rows = x_words[0].rearrange("p c t -> p (c t)").bitcast(I32)
         nc.sync.dma_start(out=wa_low[:], in_=wa_rows[:, :, low])
-        load_scale_rows(nc, xs, x_scales[0])
+        nc.sync.dma_start(out=xs[0:P:BLOCK, :].bitcast(I32), in_=x_scales[0].bitcast(I32))
         nc.sync.dma_start(out=xw[:], in_=x_rows)
         nc.sync.dma_start(out=wa_high[:], in_=wa_rows[:, :, high])
         nc.sync.dma_start(la_sb[:], la)
         nc.sync.dma_start(lb_sb[:], lb)
+
+        xw_dealt = keep.tile([P, S], I32, name="xw_dealt", align_bytes=64)
+        nc.vector.tensor_copy(xs_picked[:].rearrange("p (t m) -> p m t", t=PACK), xs[:].indirect(offs_sb[:]))
+        for r in range(PACK):
+            nc.scalar.dma_start(out=xs_dealt[r:P:QUAD, :].bitcast(I32), in_=xs_picked[BLOCK * r : P : QUAD, :].bitcast(I32))
+        w1w = late.tile([P, N], I32, name="w1w", align_bytes=64, offset=0)
+        gt_sb = late.tile([P, PACK], F32, name="gt_sb", align_bytes=64, offset=4 * N)
+        w1s = late.tile([P, N], U8, name="w1s", align_bytes=64, offset=4 * N + 64)
+        nc.gpsimd.memset(w1s[:].bitcast(I32), 0)
         nc.sync.dma_start(out=gt_sb[:], in_=gt.rearrange("(p t) o -> p (t o)", t=PACK))
         nc.sync.dma_start(out=w1w[:], in_=w1_words[0].rearrange("p c t -> p (c t)").bitcast(I32))
         load_scale_rows(nc, w1s, w1_scales[0])
-
-        xs_dealt = keep.tile([P, S], U8, name="xs_dealt", align_bytes=64)
-        xw_dealt = keep.tile([P, S], I32, name="xw_dealt", align_bytes=64)
-        nc.vector.tensor_copy(xs_dealt[:].rearrange("p (t m) -> p m t", t=PACK), xs[:].indirect(offs_sb[:]))
         nc.vector.tensor_copy(
             xw_dealt[:].bitcast(U32).rearrange("p (t m) -> p m t", t=PACK), xw[:].bitcast(U32).indirect(offs_sb[:])
         )
@@ -147,8 +154,12 @@ def tile_picked_mixscat_relu_po_kernel(
         a_tiles, b_tiles, larger, smaller, zs_tiles = {}, {}, {}, {}, {}
 
         def fetch(slot):
-            a_tiles[slot] = keep.tile([P, V], F32, name="a%d" % slot)
-            b_tiles[slot] = keep.tile([P, V], F32, align_bytes=64, name="b%d" % slot)
+            if slot == last:
+                a_tiles[slot] = pair.tile([P, V], F32, align_bytes=64, name="a%d" % slot, offset=0)
+                b_tiles[slot] = pair.tile([P, V], F32, align_bytes=64, name="b%d" % slot, offset=4 * V)
+            else:
+                a_tiles[slot] = keep.tile([P, V], F32, name="a%d" % slot)
+                b_tiles[slot] = keep.tile([P, V], F32, align_bytes=64, name="b%d" % slot)
             nc.scalar.activation(a_tiles[slot][:], y_tiles[slot][:].indirect(la_sb[:]), ACT.Copy)
             if slot == first:
                 nc.vector.tensor_copy(b_tiles[slot][:], y_tiles[slot][:].indirect(lb_sb[:]))
@@ -170,10 +181,11 @@ def tile_picked_mixscat_relu_po_kernel(
                 wide = shared.tile([P, CHUNKS * V], F32, name="gap_wide", align_bytes=64, offset=z_base)
                 gap = wide[:, :V]
             else:
-                own = keep.tile([P, V], F32, name="gap%d" % slot, tag="larger%d" % first)
+                own = pair.tile([P, V], F32, align_bytes=64, name="gap%d" % slot, offset=2 * V)
                 gap = own[:]
             up_tiles[slot] = keep.tile([P, V], F32, align_bytes=64, name="up%d" % slot)
-            larger[slot] = keep.tile([P, V], F32, name="larger%d" % slot)
+            larger_tag = "up%d" % second if slot == last else "larger%d" % slot
+            larger[slot] = keep.tile([P, V], F32, name="larger%d" % slot, tag=larger_tag, align_bytes=64)
             nc.gpsimd.tensor_tensor(gap, b_tiles[slot][:], a_tiles[slot][:], ALU.subtract)
             nc.scalar.activation(up_tiles[slot][:], gap, ACT.Relu)
             nc.gpsimd.tensor_tensor(larger[slot][:], a_tiles[slot][:], up_tiles[slot][:], ALU.add)
@@ -218,8 +230,10 @@ def tile_picked_mixscat_relu_po_kernel(
                 project(slot, cols)
             fetch(slot)
             add_larger(slot)
-        add_smaller(second, "a%d" % third)
-        add_smaller(third, "a%d" % last)
+            if slot == third:
+                add_smaller(second, "a%d" % third)
+        smaller[third] = pair.tile([P, V], F32, align_bytes=64, name="smaller%d" % third, offset=0)
+        nc.gpsimd.tensor_tensor(smaller[third][:], b_tiles[third][:], up_tiles[third][:], ALU.subtract)
         weigh(first)
         add_smaller(last, "zs%d" % first)
         w1w_dealt = keep.tile([P, N], I32, name="w1w_dealt", tag="b%d" % third, align_bytes=64)

@@ -70,6 +70,7 @@ def tile_picked_mixscat_relu_po_kernel(
         keep = ctx.enter_context(tc.tile_pool(name="keep", bufs=1))
         shared = ctx.enter_context(tc.tile_pool(name="shared", bufs=1))
         pair = ctx.enter_context(tc.tile_pool(name="pair", bufs=1))
+        chain = ctx.enter_context(tc.tile_pool(name="chain", bufs=1))
         psum = ctx.enter_context(tc.psum_pool(name="psum", bufs=8))
 
         offs_sb = keep.tile([P, S // 16], U16, name="offs_sb")
@@ -86,6 +87,10 @@ def tile_picked_mixscat_relu_po_kernel(
 
         nc.vector.memset(xs[:].bitcast(I32), 0)
         nc.gpsimd.memset(xs_dealt[:].bitcast(I32), 0)
+        p_second = keep.tile([P, H], F32, name="p_second", align_bytes=64)
+        zs_second = keep.tile([P, H], F32, name="zs_second", align_bytes=64)
+        nc.vector.memset(p_second[:], 0.0)
+        nc.vector.memset(zs_second[:], 0.0)
 
         wa_rows = wa.rearrange("(p t) c -> p t c", t=PACK)
         nc.sync.dma_start(offs_sb[:], offs)
@@ -156,7 +161,7 @@ def tile_picked_mixscat_relu_po_kernel(
         def fetch(slot):
             if slot == last:
                 a_tiles[slot] = pair.tile([P, V], F32, align_bytes=64, name="a%d" % slot, offset=0)
-                b_tiles[slot] = pair.tile([P, V], F32, align_bytes=64, name="b%d" % slot, offset=4 * V)
+                b_tiles[slot] = pair.tile([P, V], F32, align_bytes=64, name="b%d" % slot, offset=4 * H)
             else:
                 a_tiles[slot] = keep.tile([P, V], F32, name="a%d" % slot)
                 b_tiles[slot] = keep.tile([P, V], F32, align_bytes=64, name="b%d" % slot)
@@ -181,10 +186,13 @@ def tile_picked_mixscat_relu_po_kernel(
                 wide = shared.tile([P, CHUNKS * V], F32, name="gap_wide", align_bytes=64, offset=z_base)
                 gap = wide[:, :V]
             else:
-                own = pair.tile([P, V], F32, align_bytes=64, name="gap%d" % slot, offset=2 * V)
+                own = pair.tile([P, V], F32, align_bytes=64, name="gap%d" % slot, offset=4 * H)
                 gap = own[:]
-            up_tiles[slot] = keep.tile([P, V], F32, align_bytes=64, name="up%d" % slot)
-            larger_tag = "up%d" % second if slot == last else "larger%d" % slot
+            if slot == third:
+                up_tiles[slot] = chain.tile([P, V], F32, align_bytes=64, name="up%d" % slot, offset=4 * H)
+            else:
+                up_tiles[slot] = keep.tile([P, V], F32, align_bytes=64, name="up%d" % slot)
+            larger_tag = "larger%d" % slot
             larger[slot] = keep.tile([P, V], F32, name="larger%d" % slot, tag=larger_tag, align_bytes=64)
             nc.gpsimd.tensor_tensor(gap, b_tiles[slot][:], a_tiles[slot][:], ALU.subtract)
             nc.scalar.activation(up_tiles[slot][:], gap, ACT.Relu)
@@ -195,11 +203,17 @@ def tile_picked_mixscat_relu_po_kernel(
             nc.gpsimd.tensor_tensor(smaller[slot][:], b_tiles[slot][:], up_tiles[slot][:], ALU.subtract)
 
         def put_larger(slot):
-            zs_tiles[slot] = keep.tile([P, H], F32, name="zs%d" % slot)
+            if slot == first:
+                zs_tiles[slot] = chain.tile([P, H], F32, name="zs%d" % slot, align_bytes=64, offset=0)
+            elif slot == second:
+                zs_tiles[slot] = zs_second
+            else:
+                zs_tiles[slot] = keep.tile([P, H], F32, name="zs%d" % slot)
             nc.vector.tensor_copy(zs_tiles[slot][:].indirect(lb_sb[:]), larger[slot][:])
 
         def put_smaller(slot):
-            nc.vector.tensor_copy(zs_tiles[slot][:].indirect(la_sb[:]), smaller[slot][:])
+            window = p_second if slot == second else zs_tiles[slot]
+            nc.vector.tensor_copy(window[:].indirect(la_sb[:]), smaller[slot][:])
 
         def weigh(slot):
             weight = gt_sb[:, slot : slot + 1]
@@ -225,17 +239,22 @@ def tile_picked_mixscat_relu_po_kernel(
         put_larger(second)
         up_tiles[second] = keep.tile([P, V], F32, align_bytes=64, name="up%d" % second)
         nc.gpsimd.tensor_tensor(up_tiles[second][:], larger[second][:], a_tiles[second][:], ALU.subtract)
+        add_smaller(second, "smaller%d" % second)
+        put_smaller(second)
         for slot in (third, last):
             for cols in HALF_COLS:
                 project(slot, cols)
             fetch(slot)
             add_larger(slot)
-            if slot == third:
-                add_smaller(second, "a%d" % third)
-        smaller[third] = pair.tile([P, V], F32, align_bytes=64, name="smaller%d" % third, offset=0)
+            put_larger(slot)
+        joined = pair.tile([P, H], F32, align_bytes=64, name="joined", offset=0)
+        nc.gpsimd.tensor_tensor(joined[:], zs_tiles[second][:], p_second[:], ALU.add)
+        zs_tiles[second] = joined
+        smaller[third] = keep.tile([P, V], F32, align_bytes=64, name="smaller%d" % third, tag="p_second")
         nc.gpsimd.tensor_tensor(smaller[third][:], b_tiles[third][:], up_tiles[third][:], ALU.subtract)
         weigh(first)
-        add_smaller(last, "zs%d" % first)
+        smaller[last] = chain.tile([P, V], F32, align_bytes=64, name="smaller%d" % last, offset=4 * H - 2 * V)
+        nc.gpsimd.tensor_tensor(smaller[last][:], b_tiles[last][:], up_tiles[last][:], ALU.subtract)
         w1w_dealt = keep.tile([P, N], I32, name="w1w_dealt", tag="b%d" % third, align_bytes=64)
         dealt_view, plain_view = deal_views(w1w_dealt[:].bitcast(U32), w1w[:].bitcast(U32))
         nc.scalar.copy(dealt_view, plain_view)
@@ -243,9 +262,6 @@ def tile_picked_mixscat_relu_po_kernel(
         nc.gpsimd.tensor_copy(
             w1s_dealt[:].rearrange("p (t m) -> p t m", t=PACK), w1s[:].rearrange("p (m t) -> p t m", t=PACK)
         )
-        put_larger(third)
-        put_smaller(second)
-        put_larger(last)
         put_smaller(third)
         put_smaller(last)
         for slot in SLOT_ORDER[1:]:

@@ -306,14 +306,14 @@ def tile_picked_mixscat_relu_po_kernel(
             store(0, pair)
         quantise_out(0)
         quantise_out(1)
+        nc.sync.dma_start(out=out_words[:, low], in_=o_codes[:, low])
         for pair in range(2):
             mix(2, pair)
-        quantise_out(2)
-        for pair in range(2):
             mix(3, pair)
             store(1, pair)
+        quantise_out(2)
         quantise_out(3)
-        nc.sync.dma_start(out=out_words, in_=o_codes[:])
+        nc.sync.dma_start(out=out_words[:, high], in_=o_codes[:, high])
         for r in range(PACK):
             queue = nc.scalar if r % 2 == 0 else nc.sync
             queue.dma_start(out=out_2[0, r::PACK, :].bitcast(I32), in_=o_scales[r:P:QUAD, :].bitcast(I32))

@@ -71,7 +71,7 @@ def tile_picked_mixscat_relu_po_kernel(
         shared = ctx.enter_context(tc.tile_pool(name="shared", bufs=1))
         pair = ctx.enter_context(tc.tile_pool(name="pair", bufs=1))
         chain = ctx.enter_context(tc.tile_pool(name="chain", bufs=1))
-        psum = ctx.enter_context(tc.psum_pool(name="psum", bufs=8))
+        psum = ctx.enter_context(tc.psum_pool(name="psum", bufs=1))
 
         offs_sb = keep.tile([P, S // 16], U16, name="offs_sb")
         la_sb = keep.tile([P, V // 16], U16, name="la_sb")
@@ -142,11 +142,11 @@ def tile_picked_mixscat_relu_po_kernel(
             last: keep.tile([P, H], F32, name="y_last"),
         }
 
-        def project(slot, cols):
-            bank = psum.tile([P, cols.stop - cols.start], F32, name="bank", tag="bank")
+        def project(slot, cols, bank_number):
+            bank = psum.tile([P, cols.stop - cols.start], F32, name="y_bank", tag="bank%d" % bank_number)
             slot_scales = xs_dealt[:, slot_cols(slot)]
             multiply(nc, bank[:], xw_dealt[:, slot_cols(slot)], slot_scales, wa_codes[:, cols], wa_scales[:, cols])
-            if slot == second and cols == low:
+            if slot == second:
                 nc.vector.tensor_scalar(y_tiles[slot][:, cols], bank[:], 0.0, None, ALU.max)
             else:
                 nc.scalar.activation(y_tiles[slot][:, cols], bank[:], ACT.Relu)
@@ -216,7 +216,7 @@ def tile_picked_mixscat_relu_po_kernel(
             nc.vector.tensor_copy(window[:].indirect(la_sb[:]), smaller[slot][:])
 
         def weigh(slot):
-            weight = gt_sb[:, slot : slot + 1]
+            weight = gt_third[:] if slot == third else gt_sb[:, slot : slot + 1]
             for q in range(CHUNKS):
                 zs_chunk = zs_tiles[slot][:, CHUNK_COLS[q]]
                 if slot == last and q < CHUNKS // 2:
@@ -224,12 +224,12 @@ def tile_picked_mixscat_relu_po_kernel(
                 else:
                     nc.scalar.activation(z_grouped[q][:, :, slot], zs_chunk, ACT.Copy, scale=weight)
 
-        project(first, low)
-        project(second, low)
-        project(first, CHUNK_COLS[3])
-        project(first, CHUNK_COLS[2])
+        project(first, low, 0)
+        project(second, low, 1)
+        project(first, CHUNK_COLS[3], 2)
+        project(first, CHUNK_COLS[2], 3)
         fetch(first)
-        project(second, high)
+        project(second, high, 2)
         fetch(second)
         take_larger(first)
         take_smaller(first, keep)
@@ -241,17 +241,19 @@ def tile_picked_mixscat_relu_po_kernel(
         nc.gpsimd.tensor_tensor(up_tiles[second][:], larger[second][:], a_tiles[second][:], ALU.subtract)
         add_smaller(second, "smaller%d" % second)
         put_smaller(second)
-        for slot in (third, last):
+        for slot, bank_number in ((third, 3), (last, 2)):
             for cols in HALF_COLS:
-                project(slot, cols)
+                project(slot, cols, bank_number)
             fetch(slot)
             add_larger(slot)
             put_larger(slot)
-        joined = pair.tile([P, H], F32, align_bytes=64, name="joined", offset=0)
+        smaller[third] = pair.tile([P, V], F32, align_bytes=64, name="smaller%d" % third, offset=0)
+        nc.gpsimd.tensor_tensor(smaller[third][:], b_tiles[third][:], up_tiles[third][:], ALU.subtract)
+        joined = chain.tile([P, H], F32, align_bytes=64, name="joined", offset=4 * H + 2 * V)
         nc.gpsimd.tensor_tensor(joined[:], zs_tiles[second][:], p_second[:], ALU.add)
         zs_tiles[second] = joined
-        smaller[third] = keep.tile([P, V], F32, align_bytes=64, name="smaller%d" % third, tag="p_second")
-        nc.gpsimd.tensor_tensor(smaller[third][:], b_tiles[third][:], up_tiles[third][:], ALU.subtract)
+        gt_third = keep.tile([P, 1], F32, align_bytes=64, name="gt_third", tag="p_second")
+        nc.scalar.copy(gt_third[:], gt_sb[:, third : third + 1])
         weigh(first)
         smaller[last] = chain.tile([P, V], F32, align_bytes=64, name="smaller%d" % last, offset=4 * H - 2 * V)
         nc.gpsimd.tensor_tensor(smaller[last][:], b_tiles[last][:], up_tiles[last][:], ALU.subtract)
@@ -278,7 +280,7 @@ def tile_picked_mixscat_relu_po_kernel(
         o_halves = [keep.tile([P, PACK, H // 2], F32, name="o_half%d" % h, align_bytes=64) for h in range(2)]
 
         def mix(q, pair):
-            bank = psum.tile([P, 2, CW], F32, name="bank", tag="bank")
+            bank = psum.tile([P, 2, CW], F32, name="o_bank", tag="bank%d" % (2 * q + pair))
             for place in range(2):
                 slot = 2 * pair + place
                 multiply(

@@ -105,7 +105,7 @@ def tile_picked_mixscat_relu_po_kernel(
         xw_dealt = keep.tile([P, S], I32, name="xw_dealt", align_bytes=64)
         nc.vector.tensor_copy(xs_picked[:].rearrange("p (t m) -> p m t", t=PACK), xs[:].indirect(offs_sb[:]))
         for r in range(PACK):
-            nc.scalar.dma_start(out=xs_dealt[r:P:QUAD, :].bitcast(I32), in_=xs_picked[BLOCK * r : P : QUAD, :].bitcast(I32))
+            nc.sync.dma_start(out=xs_dealt[r:P:QUAD, :].bitcast(I32), in_=xs_picked[BLOCK * r : P : QUAD, :].bitcast(I32))
         w1w = late.tile([P, N], I32, name="w1w", align_bytes=64, offset=0)
         gt_sb = late.tile([P, PACK], F32, name="gt_sb", align_bytes=64, offset=4 * N)
         w1s = late.tile([P, N], U8, name="w1s", align_bytes=64, offset=4 * N + 64)

@@ -93,9 +93,9 @@ def tile_picked_mixscat_relu_po_kernel(
         nc.vector.memset(zs_second[:], 0.0)
 
         wa_rows = wa.rearrange("(p t) c -> p t c", t=PACK)
-        nc.sync.dma_start(offs_sb[:], offs)
         x_rows = x_words[0].rearrange("p c t -> p (c t)").bitcast(I32)
         nc.sync.dma_start(out=wa_low[:], in_=wa_rows[:, :, low])
+        nc.sync.dma_start(offs_sb[:], offs)
         nc.sync.dma_start(out=xs[0:P:BLOCK, :].bitcast(I32), in_=x_scales[0].bitcast(I32))
         nc.sync.dma_start(out=xw[:], in_=x_rows)
         nc.sync.dma_start(out=wa_high[:], in_=wa_rows[:, :, high])

@@ -317,5 +317,5 @@ def tile_picked_mixscat_relu_po_kernel(
         quantise_out(3)
         nc.sync.dma_start(out=out_words[:, high], in_=o_codes[:, high])
         for r in range(PACK):
-            queue = nc.scalar if r % 2 == 0 else nc.sync
+            queue = nc.scalar if r == 0 else nc.sync
             queue.dma_start(out=out_2[0, r::PACK, :].bitcast(I32), in_=o_scales[r:P:QUAD, :].bitcast(I32))

from contextlib import ExitStack

import concourse.mybir as mybir

K, T, S, V, N, H = 512, 2048, 512, 256, 512, 512
FLOPS = 2 * K * S * H + 2 * S * N * H

F32 = mybir.dt.float32
BF16 = mybir.dt.bfloat16
I32 = mybir.dt.int32
U32 = mybir.dt.uint32
U16 = mybir.dt.uint16
U8 = mybir.dt.uint8
FP8X4 = mybir.dt.float8_e4m3fn_x4
ALU = mybir.AluOpType
ACT = mybir.ActivationFunctionType

P = 128
PACK = 4
QUAD = 32
BLOCK = 8
LINE = 4
CW = 128
CHUNKS = H // CW
CHUNK_COLS = [slice(q * CW, (q + 1) * CW) for q in range(CHUNKS)]
HALF_COLS = [slice(0, H // 2), slice(H // 2, H)]
SLOT_ORDER = (2, 0, 1, 3)


def load_scale_rows(nc, plane, rows):
    for r in range(PACK):
        nc.sync.dma_start(out=plane[r:P:QUAD, :].bitcast(I32), in_=rows[r::PACK, :].bitcast(I32))


def deal_views(dealt, plain):
    return dealt.rearrange("p (t m) -> p m t", t=PACK), plain.rearrange("p (m t) -> p m t", t=PACK)


def interleave_views(grouped, slots):
    return grouped.rearrange("p (c i) t -> p c t i", i=LINE), slots.rearrange("p t (c i) -> p c t i", i=LINE)


def quantise(nc, codes, scales, grouped):
    nc.vector.quantize_mx(out=codes.bitcast(FP8X4), scales=scales, in_=grouped.rearrange("p c t -> p (c t)"))


def multiply(nc, out, left_codes, left_scales, right_codes, right_scales):
    nc.tensor.matmul_mx(
        out=out,
        lhsT=left_codes.bitcast(FP8X4),
        lhsT_scale=left_scales,
        rhs=right_codes.bitcast(FP8X4),
        rhs_scale=right_scales,
        start=True,
        stop=True,
    )


def slot_cols(slot):
    return slice(slot * P, (slot + 1) * P)


def tile_picked_mixscat_relu_po_kernel(
    tc, x_words, x_scales, wa, gt, w1_words, w1_scales, offs, la, lb, out_0, out_1, out_2
):
    nc = tc.nc
    first, second, third, last = SLOT_ORDER
    low, high = HALF_COLS
    with ExitStack() as ctx:
        keep = ctx.enter_context(tc.tile_pool(name="keep", bufs=1))
        shared = ctx.enter_context(tc.tile_pool(name="shared", bufs=1))
        pair = ctx.enter_context(tc.tile_pool(name="pair", bufs=1))
        chain = ctx.enter_context(tc.tile_pool(name="chain", bufs=1))
        psum = ctx.enter_context(tc.psum_pool(name="psum", bufs=1))

        offs_sb = keep.tile([P, S // 16], U16, name="offs_sb")
        la_sb = keep.tile([P, V // 16], U16, name="la_sb")
        lb_sb = keep.tile([P, V // 16], U16, name="lb_sb")
        xw = keep.tile([P, T], I32, name="xw", align_bytes=64)
        xs = keep.tile([P, T], U8, name="xs", align_bytes=64)
        wa_low = keep.tile([P, PACK, H // 2], F32, name="wa_low", align_bytes=64)
        wa_high = shared.tile([P, PACK, H // 2], F32, name="wa_high", align_bytes=64, offset=0)
        late = ctx.enter_context(tc.tile_pool(name="late", bufs=1))
        picked_at = 4 * N - 64
        xs_picked = late.tile([P, S], U8, name="xs_picked", align_bytes=64, offset=picked_at)
        xs_dealt = keep.tile([P, S], U8, name="xs_dealt", align_bytes=64)

        nc.vector.memset(xs[:].bitcast(I32), 0)
        nc.gpsimd.memset(xs_dealt[:].bitcast(I32), 0)
        p_second = keep.tile([P, H], F32, name="p_second", align_bytes=64)
        zs_second = keep.tile([P, H], F32, name="zs_second", align_bytes=64)
        nc.vector.memset(p_second[:], 0.0)
        nc.vector.memset(zs_second[:], 0.0)

        wa_rows = wa.rearrange("(p t) c -> p t c", t=PACK)
        x_rows = x_words[0].rearrange("p c t -> p (c t)").bitcast(I32)
        nc.sync.dma_start(out=wa_low[:], in_=wa_rows[:, :, low])
        nc.sync.dma_start(offs_sb[:], offs)
        nc.sync.dma_start(out=xs[0:P:BLOCK, :].bitcast(I32), in_=x_scales[0].bitcast(I32))
        nc.sync.dma_start(out=xw[:], in_=x_rows)
        nc.sync.dma_start(out=wa_high[:], in_=wa_rows[:, :, high])
        nc.sync.dma_start(la_sb[:], la)
        nc.sync.dma_start(lb_sb[:], lb)

        xw_dealt = keep.tile([P, S], I32, name="xw_dealt", align_bytes=64)
        nc.vector.tensor_copy(xs_picked[:].rearrange("p (t m) -> p m t", t=PACK), xs[:].indirect(offs_sb[:]))
        for r in range(PACK):
            nc.sync.dma_start(out=xs_dealt[r:P:QUAD, :].bitcast(I32), in_=xs_picked[BLOCK * r : P : QUAD, :].bitcast(I32))
        w1w = late.tile([P, N], I32, name="w1w", align_bytes=64, offset=0)
        gt_sb = late.tile([P, PACK], F32, name="gt_sb", align_bytes=64, offset=4 * N)
        w1s = late.tile([P, N], U8, name="w1s", align_bytes=64, offset=4 * N + 64)
        nc.gpsimd.memset(w1s[:].bitcast(I32), 0)
        nc.sync.dma_start(out=gt_sb[:], in_=gt.rearrange("(p t) o -> p (t o)", t=PACK))
        nc.sync.dma_start(out=w1w[:], in_=w1_words[0].rearrange("p c t -> p (c t)").bitcast(I32))
        load_scale_rows(nc, w1s, w1_scales[0])
        nc.vector.tensor_copy(
            xw_dealt[:].bitcast(U32).rearrange("p (t m) -> p m t", t=PACK), xw[:].bitcast(U32).indirect(offs_sb[:])
        )

        wa_codes = keep.tile([P, H], I32, name="wa_codes", align_bytes=64)
        wa_scales = keep.tile([P, H], U8, name="wa_scales", align_bytes=64)
        half_chunk = CW // 2
        wa_pieces = (
            (nc.scalar.copy, wa_low[:], low, "wa_grouped_low"),
            (nc.vector.tensor_copy, wa_high[:, :, CW : CW + half_chunk], slice(H - CW, H - half_chunk), "wa_grouped3a"),
            (nc.vector.tensor_copy, wa_high[:, :, CW + half_chunk :], slice(H - half_chunk, H), "wa_grouped3b"),
            (nc.scalar.copy, wa_high[:, :, :CW], CHUNK_COLS[2], "wa_grouped2"),
        )
        for pieces in (wa_pieces[:1], wa_pieces[1:]):
            rounded = []
            for cast, piece, cols, tag in pieces:
                grouped = keep.tile([P, cols.stop - cols.start, PACK], BF16, name=tag, align_bytes=64)
                cast(*interleave_views(grouped[:], piece))
                rounded.append((cols, grouped))
            for cols, grouped in rounded:
                quantise(nc, wa_codes[:, cols], wa_scales[:, cols], grouped[:])

        y_tiles = {
            first: shared.tile([P, H], F32, name="y_first", align_bytes=64, offset=0),
            second: shared.tile([P, H], F32, name="y_second", align_bytes=64, offset=4 * H),
            third: keep.tile([P, H], F32, name="y_third"),
            last: keep.tile([P, H], F32, name="y_last"),
        }

        def project(slot, cols, bank_number):
            bank = psum.tile([P, cols.stop - cols.start], F32, name="y_bank", tag="bank%d" % bank_number)
            slot_scales = xs_dealt[:, slot_cols(slot)]
            multiply(nc, bank[:], xw_dealt[:, slot_cols(slot)], slot_scales, wa_codes[:, cols], wa_scales[:, cols])
            if slot == second:
                nc.vector.tensor_scalar(y_tiles[slot][:, cols], bank[:], 0.0, None, ALU.max)
            else:
                nc.scalar.activation(y_tiles[slot][:, cols], bank[:], ACT.Relu)

        z_base = 2 * 4 * H
        z_grouped = [
            shared.tile([P, CW, PACK], BF16, name="z_grouped%d" % q, align_bytes=64, offset=z_base + q * 2 * PACK * CW)
            for q in range(CHUNKS)
        ]
        a_tiles, b_tiles, larger, smaller, zs_tiles = {}, {}, {}, {}, {}

        def fetch(slot):
            if slot == last:
                a_tiles[slot] = pair.tile([P, V], F32, align_bytes=64, name="a%d" % slot, offset=0)
                b_tiles[slot] = pair.tile([P, V], F32, align_bytes=64, name="b%d" % slot, offset=4 * H)
            else:
                a_tiles[slot] = keep.tile([P, V], F32, name="a%d" % slot)
                b_tiles[slot] = keep.tile([P, V], F32, align_bytes=64, name="b%d" % slot)
            nc.scalar.activation(a_tiles[slot][:], y_tiles[slot][:].indirect(la_sb[:]), ACT.Copy)
            if slot == first:
                nc.vector.tensor_copy(b_tiles[slot][:], y_tiles[slot][:].indirect(lb_sb[:]))
            else:
                nc.scalar.activation(b_tiles[slot][:], y_tiles[slot][:].indirect(lb_sb[:]), ACT.Copy)

        def take_larger(slot):
            larger[slot] = keep.tile([P, V], F32, name="larger%d" % slot)
            nc.vector.tensor_tensor(larger[slot][:], a_tiles[slot][:], b_tiles[slot][:], ALU.max)

        def take_smaller(slot, pool, **place):
            smaller[slot] = pool.tile([P, V], F32, name="smaller%d" % slot, **place)
            nc.vector.tensor_tensor(smaller[slot][:], a_tiles[slot][:], b_tiles[slot][:], ALU.min)

        up_tiles = {}

        def add_larger(slot):
            if slot == last:
                wide = shared.tile([P, CHUNKS * V], F32, name="gap_wide", align_bytes=64, offset=z_base)
                gap = wide[:, :V]
            else:
                own = pair.tile([P, V], F32, align_bytes=64, name="gap%d" % slot, offset=4 * H)
                gap = own[:]
            if slot == third:
                up_tiles[slot] = chain.tile([P, V], F32, align_bytes=64, name="up%d" % slot, offset=4 * H)
            else:
                up_tiles[slot] = keep.tile([P, V], F32, align_bytes=64, name="up%d" % slot)
            larger_tag = "larger%d" % slot
            larger[slot] = keep.tile([P, V], F32, name="larger%d" % slot, tag=larger_tag, align_bytes=64)
            nc.gpsimd.tensor_tensor(gap, b_tiles[slot][:], a_tiles[slot][:], ALU.subtract)
            nc.scalar.activation(up_tiles[slot][:], gap, ACT.Relu)
            nc.gpsimd.tensor_tensor(larger[slot][:], a_tiles[slot][:], up_tiles[slot][:], ALU.add)

        def add_smaller(slot, tag):
            smaller[slot] = keep.tile([P, V], F32, name="smaller%d" % slot, tag=tag)
            nc.gpsimd.tensor_tensor(smaller[slot][:], b_tiles[slot][:], up_tiles[slot][:], ALU.subtract)

        def put_larger(slot):
            if slot == first:
                zs_tiles[slot] = chain.tile([P, H], F32, name="zs%d" % slot, align_bytes=64, offset=0)
            elif slot == second:
                zs_tiles[slot] = zs_second
            else:
                zs_tiles[slot] = keep.tile([P, H], F32, name="zs%d" % slot)
            nc.vector.tensor_copy(zs_tiles[slot][:].indirect(lb_sb[:]), larger[slot][:])

        def put_smaller(slot):
            window = p_second if slot == second else zs_tiles[slot]
            nc.vector.tensor_copy(window[:].indirect(la_sb[:]), smaller[slot][:])

        def weigh(slot):
            weight = gt_third[:] if slot == third else gt_sb[:, slot : slot + 1]
            for q in range(CHUNKS):
                zs_chunk = zs_tiles[slot][:, CHUNK_COLS[q]]
                if slot == last and q < CHUNKS // 2:
                    nc.vector.tensor_scalar(z_grouped[q][:, :, slot], zs_chunk, weight, None, ALU.mult)
                else:
                    nc.scalar.activation(z_grouped[q][:, :, slot], zs_chunk, ACT.Copy, scale=weight)

        project(first, low, 0)
        project(second, low, 1)
        project(first, CHUNK_COLS[3], 2)
        project(first, CHUNK_COLS[2], 3)
        fetch(first)
        project(second, high, 2)
        fetch(second)
        take_larger(first)
        take_smaller(first, keep)
        put_larger(first)
        take_larger(second)
        put_smaller(first)
        put_larger(second)
        up_tiles[second] = keep.tile([P, V], F32, align_bytes=64, name="up%d" % second)
        nc.gpsimd.tensor_tensor(up_tiles[second][:], larger[second][:], a_tiles[second][:], ALU.subtract)
        add_smaller(second, "smaller%d" % second)
        put_smaller(second)
        for slot, bank_number in ((third, 3), (last, 2)):
            for cols in HALF_COLS:
                project(slot, cols, bank_number)
            fetch(slot)
            add_larger(slot)
            put_larger(slot)
        smaller[third] = pair.tile([P, V], F32, align_bytes=64, name="smaller%d" % third, offset=0)
        nc.gpsimd.tensor_tensor(smaller[third][:], b_tiles[third][:], up_tiles[third][:], ALU.subtract)
        joined = chain.tile([P, H], F32, align_bytes=64, name="joined", offset=4 * H + 2 * V)
        nc.gpsimd.tensor_tensor(joined[:], zs_tiles[second][:], p_second[:], ALU.add)
        zs_tiles[second] = joined
        gt_third = keep.tile([P, 1], F32, align_bytes=64, name="gt_third", tag="p_second")
        nc.scalar.copy(gt_third[:], gt_sb[:, third : third + 1])
        weigh(first)
        smaller[last] = chain.tile([P, V], F32, align_bytes=64, name="smaller%d" % last, offset=4 * H - 2 * V)
        nc.gpsimd.tensor_tensor(smaller[last][:], b_tiles[last][:], up_tiles[last][:], ALU.subtract)
        w1w_dealt = keep.tile([P, N], I32, name="w1w_dealt", tag="b%d" % third, align_bytes=64)
        dealt_view, plain_view = deal_views(w1w_dealt[:].bitcast(U32), w1w[:].bitcast(U32))
        nc.scalar.copy(dealt_view, plain_view)
        w1s_dealt = keep.tile([P, N], U8, name="w1s_dealt", tag="up%d" % last, align_bytes=64)
        nc.gpsimd.tensor_copy(
            w1s_dealt[:].rearrange("p (t m) -> p t m", t=PACK), w1s[:].rearrange("p (m t) -> p t m", t=PACK)
        )
        put_smaller(third)
        put_smaller(last)
        for slot in SLOT_ORDER[1:]:
            weigh(slot)

        z_codes = keep.tile([P, H], I32, name="z_codes", align_bytes=64)
        z_scales = keep.tile([P, H], U8, name="z_scales", align_bytes=64)
        o_codes = keep.tile([P, H], I32, name="o_codes", align_bytes=64)
        o_scales = keep.tile([P, H], U8, name="o_scales", align_bytes=64)
        out_rows = out_0.rearrange("(p t) c -> p t c", t=PACK)
        out_words = out_1[0].rearrange("p c t -> p (c t)").bitcast(I32)
        for q in range(CHUNKS):
            quantise(nc, z_codes[:, CHUNK_COLS[q]], z_scales[:, CHUNK_COLS[q]], z_grouped[q][:])
        o_halves = [keep.tile([P, PACK, H // 2], F32, name="o_half%d" % h, align_bytes=64) for h in range(2)]

        def mix(q, pair):
            bank = psum.tile([P, 2, CW], F32, name="o_bank", tag="bank%d" % (2 * q + pair))
            for place in range(2):
                slot = 2 * pair + place
                multiply(
                    nc,
                    bank[:, place, :],
                    w1w_dealt[:, slot_cols(slot)],
                    w1s_dealt[:, slot_cols(slot)],
                    z_codes[:, CHUNK_COLS[q]],
                    z_scales[:, CHUNK_COLS[q]],
                )
            nc.scalar.copy(o_halves[q // 2][:, 2 * pair : 2 * pair + 2, CHUNK_COLS[q % 2]], bank[:])

        def store(h, pair):
            places = slice(2 * pair, 2 * pair + 2)
            nc.sync.dma_start(out=out_rows[:, places, HALF_COLS[h]], in_=o_halves[h][:, places, :])

        def quantise_out(q):
            o_grouped = keep.tile([P, CW, PACK], BF16, name="o_grouped%d" % q, align_bytes=64)
            nc.vector.tensor_copy(*interleave_views(o_grouped[:], o_halves[q // 2][:, :, CHUNK_COLS[q % 2]]))
            quantise(nc, o_codes[:, CHUNK_COLS[q]], o_scales[:, CHUNK_COLS[q]], o_grouped[:])

        for pair in range(2):
            mix(0, pair)
            mix(1, pair)
            store(0, pair)
        quantise_out(0)
        quantise_out(1)
        nc.sync.dma_start(out=out_words[:, low], in_=o_codes[:, low])
        for pair in range(2):
            mix(2, pair)
            mix(3, pair)
            store(1, pair)
        quantise_out(2)
        quantise_out(3)
        nc.sync.dma_start(out=out_words[:, high], in_=o_codes[:, high])
        for r in range(PACK):
            queue = nc.scalar if r == 0 else nc.sync
            queue.dma_start(out=out_2[0, r::PACK, :].bitcast(I32), in_=o_scales[r:P:QUAD, :].bitcast(I32))
